import numpy as np
import ml_dtypes


def mxq(x, axis, fmt="e4m3"):
    dtype, down = {"e4m3": (ml_dtypes.float8_e4m3fn, 7), "e5m2": (ml_dtypes.float8_e5m2, 14)}[fmt]
    v = np.moveaxis(np.asarray(x, np.float32).astype(ml_dtypes.bfloat16).astype(np.float64), axis, -1)
    blocks = v.reshape(v.shape[:-1] + (-1, 32))
    amax = np.abs(blocks).max(-1, keepdims=True)
    byte = np.maximum(np.where(amax > 0, np.frexp(amax)[1] - 1 + 127, 0) - down, 1)
    scale = np.exp2(byte - 127.0)
    codes = (blocks / scale).astype(np.float32).astype(dtype).astype(np.float64)
    return np.moveaxis((codes * scale).reshape(v.shape), -1, axis)


WIDE = False


def mx_kscale(k):
    if not WIDE:
        return np.ones(k)
    levels = np.array([10, -10, 5, -5, 0])
    if k % 512:
        return np.exp2(np.random.permutation(np.resize(levels, k // 32))).repeat(32)
    a = np.empty((k // 512, 16))
    for p in range(k // 512):
        a[p, :8] = np.random.permutation(np.resize(levels, 8))
        for g in range(8):
            far = levels[np.abs(levels - a[p, g]) >= 10]
            a[p, g + 8] = far[np.random.randint(len(far))]
    return np.exp2(a.ravel()).repeat(32)


def f64(x):
    return np.asarray(x).astype(np.float64)


def striped(idx):
    return np.tile(idx.reshape(-1, 16).T, (8, 1)).astype(np.uint16)


def unstriped(offs):
    return offs[:16].T.reshape(-1).astype(np.int64)


E2M1 = np.array([0.0, 0.5, 1.0, 1.5, 2.0, 3.0, 4.0, 6.0, -0.0, -0.5, -1.0, -1.5, -2.0, -3.0, -4.0, -6.0])


def pack_weight(w, fmt):
    k, n = w.shape
    w = f64(np.asarray(w, np.float32).astype(ml_dtypes.bfloat16)).reshape(k // 32, 32, n)
    amax = np.abs(w).max(1)
    if fmt == "e4m3":
        byte = np.frexp(amax)[1] - 1 + 127 - 7
    else:
        mant, ex = np.frexp(amax / 6.0)
        byte = np.where(mant > 0.5, ex, ex - 1) + 127
    byte = np.clip(np.where(amax > 0, byte, 1), 1, 254)
    scaled = (w * np.exp2(127.0 - byte)[:, None, :]).reshape(k, n).astype(np.float32)
    by_word = np.ascontiguousarray(scaled.reshape(k // 512, 128, 4, n).transpose(0, 1, 3, 2))
    if fmt == "e4m3":
        words = by_word.astype(ml_dtypes.float8_e4m3fn).view(np.uint8)
    else:
        c = by_word.astype(ml_dtypes.float4_e2m1fn).view(np.uint8) & 0xF
        words = (c[..., 0::2] | (c[..., 1::2] << 4)).reshape(k // 512, 128, 2 * n)
    return np.ascontiguousarray(words), np.ascontiguousarray(byte.astype(np.uint8).reshape(k // 512, 16, n))


def unpack_weight(words, scales, fmt):
    g, _, n = scales.shape
    words = np.ascontiguousarray(words).reshape(g, 128, n, -1)
    if fmt == "e4m3":
        vals = words.view(ml_dtypes.float8_e4m3fn).astype(np.float64)
    else:
        nib = np.empty((g, 128, n, 4), np.uint8)
        nib[..., 0::2] = words & 0xF
        nib[..., 1::2] = words >> 4
        vals = E2M1[nib]
    vals = vals * np.repeat(np.exp2(scales.astype(np.float64) - 127.0), 8, axis=1)[..., None]
    return vals.transpose(0, 1, 3, 2).reshape(g * 512, n)


def gelu(v):
    return 0.5 * v * (1.0 + np.tanh(np.sqrt(2.0 / np.pi) * (v + 0.044715 * v**3)))


K, T, E, C, H, N = 1024, 1024, 8, 256, 512, 128
R = 2


def by_expert(wq, xq):
    return np.concatenate([wq[e].T @ xq[:, e * C:(e + 1) * C] for e in range(E)], axis=1)


def setup_inputs():
    n = np.random.standard_normal
    s = mx_kscale(K)[:, None]
    u = mx_kscale(H)
    slot_token = np.concatenate([r * (T // R) + np.random.permutation(T // R)[:C // R] for e in range(E) for r in range(R)])
    x = pack_weight(n((K, T)) * s, "e4m3")
    return {
        "x_words": x[0],
        "x_scales": x[1],
        "w1": (n((E, K, H)) / np.sqrt(K) / s[None] * u[None, None, :]).astype(np.float32),
        "w2": (n((E, H, N)) / np.sqrt(H) / u[None, :, None]).astype(np.float32),
        "offs": striped(slot_token),
    }


def reference(x_words, x_scales, w1, w2, offs):
    idx = unstriped(offs)
    xq = unpack_weight(x_words, x_scales, "e4m3")[:, idx]
    h = gelu(by_expert(mxq(f64(w1), 1, "e4m3"), xq))
    y = by_expert(mxq(f64(w2), 1, "e4m3"), mxq(h, 0, "e4m3"))
    return y.reshape(N, E, R, C // R).transpose(0, 2, 1, 3).reshape(N, E * C)

@@ -1,0 +1,217 @@
+from contextlib import ExitStack
+
+import concourse.mybir as mybir
+
+K, T, E, C, H, N = 1024, 1024, 8, 256, 512, 128
+R = 2
+FLOPS = 2 * E * C * (K * H + H * N)
+
+F32 = mybir.dt.float32
+BF16 = mybir.dt.bfloat16
+I32 = mybir.dt.int32
+U32 = mybir.dt.uint32
+U16 = mybir.dt.uint16
+U8 = mybir.dt.uint8
+FP8X4 = mybir.dt.float8_e4m3fn_x4
+GELU = mybir.ActivationFunctionType.Gelu_apprx_tanh
+
+P = 128
+PACK = 4
+K_PASS = P * PACK
+PASSES = K // K_PASS
+U = C // R
+LIST_COLS = C // 16
+
+EARLY = 3
+SETS = 3
+STORE_GROUPS = [(0, 1, 2), (3, 4), (5, 6), (7,)]
+
+
+def tile_moe_pke_mlp_gelu_kernel(tc, x_words, x_scales, w1, w2, offs, out):
+    nc = tc.nc
+    with ExitStack() as ctx:
+        held = ctx.enter_context(tc.tile_pool(name="held", bufs=1))
+        ring = ctx.enter_context(tc.tile_pool(name="ring", bufs=8))
+        psum_a = ctx.enter_context(tc.psum_pool(name="psum_a", bufs=4))
+        psum_y = ctx.enter_context(tc.psum_pool(name="psum_y", bufs=4))
+
+        offsets = held.tile([P, E * LIST_COLS], U16, name="offsets")
+        tok_words = [held.tile([P, T], I32, name="tok_words%d" % o, align_bytes=64) for o in range(PASSES)]
+        tok_scales = held.tile([P, T], U8, name="tok_scales", align_bytes=64)
+        w1_raw = [[held.tile([P, PACK, H], F32, name="w1_raw%d_%d" % (e, o), align_bytes=64) for o in range(PASSES)] for e in range(E)]
+        w2_early = held.tile([P, EARLY, PACK, N], F32, name="w2_early", align_bytes=64)
+        w2_raw = [w2_early[:, e, :, :] for e in range(EARLY)]
+        w2_raw += [held.tile([P, PACK, N], F32, name="w2_late%d" % e, align_bytes=64)[:] for e in range(EARLY, E)]
+        y_sb = [held.tile([P, R, len(g) * U], F32, name="y_sb%d" % g[0], align_bytes=64) for g in STORE_GROUPS]
+        stage = [held.tile([P, 2 * P * PACK], BF16, name="stage%d" % i, align_bytes=64) for i in range(3)]
+        h_stage = [held.tile([P, C * PACK], BF16, name="h_stage%d" % i, align_bytes=64) for i in range(2)]
+        w2_stage = [held.tile([P, N * PACK], BF16, name="w2_stage%d" % e, align_bytes=64) for e in range(EARLY)]
+        slot_words = [[held.tile([P, C], U32, name="slot_words%d_%d" % (s, o), align_bytes=64) for o in range(PASSES)] for s in range(SETS)]
+        slot_scales = [held.tile([P, C], U8, name="slot_scales%d" % s, align_bytes=64) for s in range(SETS)]
+        warm_in = held.tile([P, 1], F32, name="warm_in")
+        warm_out = held.tile([P, 1], F32, name="warm_out")
+
+        nc.vector.memset(warm_in[:], 0.0)
+        nc.scalar.activation(out=warm_out[:], in_=warm_in[:], func=GELU)
+        nc.vector.memset(tok_scales[:].bitcast(I32), 0)
+
+        def load_words(o):
+            nc.sync.dma_start(out=tok_words[o][:], in_=x_words[o].rearrange("p n r -> p (n r)").bitcast(I32))
+
+        nc.sync.dma_start(offsets[:], offs)
+        load_words(0)
+        for q in range(4):
+            nc.sync.dma_start(
+                out=tok_scales[32 * q : 32 * q + 4 * PASSES, :].bitcast(I32),
+                in_=x_scales[:, 4 * q : 4 * q + 4, :].bitcast(I32),
+            )
+        nc.sync.dma_start(
+            out=w2_early[:].rearrange("p e j n -> p e (j n)"),
+            in_=w2[0:EARLY].rearrange("e (p j) n -> p e (j n)", j=PACK),
+        )
+        load_words(1)
+        for e in range(E):
+            for o in range(PASSES):
+                nc.sync.dma_start(
+                    out=w1_raw[e][o][:],
+                    in_=w1[e, o * K_PASS : (o + 1) * K_PASS, :].rearrange("(p j) c -> p j c", j=PACK),
+                )
+        for e in range(EARLY, E):
+            nc.sync.dma_start(out=w2_raw[e], in_=w2[e].rearrange("(p j) n -> p j n", j=PACK))
+
+        def quantise(src, width, pool, name):
+            codes = pool.tile([P, width], U32, name=name + "_codes", align_bytes=64)
+            scales = pool.tile([P, width], U8, name=name + "_scales", align_bytes=64)
+            nc.vector.quantize_mx(out=codes[:].bitcast(FP8X4), scales=scales[:], in_=src)
+            return codes, scales
+
+        def round_w2(e, copy, dst):
+            copy(
+                out=dst.rearrange("p (c i j) -> p c j i", i=4, j=PACK),
+                in_=w2_raw[e].rearrange("p j (c i) -> p c j i", i=4),
+            )
+
+        def round_w1(e, o, pair, copy, dst):
+            src = w1_raw[e][o][:].rearrange("p j (m t) -> p m j t", t=PACK)[:, :, :, 2 * pair : 2 * pair + 2]
+            copy(out=dst.rearrange("p (t m j) -> p m j t", t=2, j=PACK), in_=src)
+
+        w1_mx = {}
+        w2_mx = {}
+        h_mx = {}
+        banks = {}
+
+        def gather_words(e, o):
+            cols = slice(e * LIST_COLS, (e + 1) * LIST_COLS)
+            nc.vector.tensor_copy(out=slot_words[e % SETS][o][:], in_=tok_words[o][:].bitcast(U32).indirect(offsets[:, cols]))
+
+        def gather_scales(e):
+            cols = slice(e * LIST_COLS, (e + 1) * LIST_COLS)
+            nc.vector.tensor_copy(out=slot_scales[e % SETS][:], in_=tok_scales[:].indirect(offsets[:, cols]))
+
+        def w1_stage(e, o, pair):
+            return stage[(2 * (PASSES * e + o) + pair) % 3]
+
+        def quantise_w1(e, o, pair):
+            w1_mx[(e, o, pair)] = quantise(w1_stage(e, o, pair)[:], 2 * P, ring, "w1")
+
+        def first_product(e):
+            words, scales = slot_words[e % SETS], slot_scales[e % SETS]
+            banks[e] = [psum_a.tile([P, PACK, U], F32, name="a_bank") for r in range(R)]
+            for pair in range(2):
+                for r in range(R):
+                    ncols = slice(r * U, (r + 1) * U)
+                    for t in (2 * pair, 2 * pair + 1):
+                        mcols = slice((t % 2) * P, (t % 2 + 1) * P)
+                        for o in range(PASSES):
+                            wc, ws = w1_mx[(e, o, pair)]
+                            nc.tensor.matmul_mx(
+                                out=banks[e][r][:, t, :],
+                                lhsT=wc[:, mcols].bitcast(FP8X4),
+                                lhsT_scale=ws[:, mcols],
+                                rhs=words[o][:, ncols].bitcast(FP8X4),
+                                rhs_scale=scales[4 * o : P, ncols],
+                                start=(o == 0),
+                                stop=(o == PASSES - 1),
+                            )
+
+        def activate(e):
+            h_bf = h_stage[e % 2]
+            for r in range(R):
+                nc.scalar.activation(
+                    out=h_bf[:, r * U * PACK : (r + 1) * U * PACK].rearrange("p (u t) -> p u t", t=PACK),
+                    in_=banks[e][r][:].rearrange("p t u -> p u t"),
+                    func=GELU,
+                )
+
+        def quantise_h(e):
+            h_mx[e] = quantise(h_stage[e % 2][:], C, held, "h%d" % e)
+
+        def second_product(e):
+            y_bank = psum_y.tile([P, R, U], F32, name="y_bank")
+            nc.tensor.matmul_mx(
+                out=y_bank[:].rearrange("p r u -> p (r u)"),
+                lhsT=w2_mx[e][0][:].bitcast(FP8X4),
+                lhsT_scale=w2_mx[e][1][:],
+                rhs=h_mx[e][0][:].bitcast(FP8X4),
+                rhs_scale=h_mx[e][1][:],
+                start=True,
+                stop=True,
+            )
+            si = [i for i, g in enumerate(STORE_GROUPS) if e in g][0]
+            sg = STORE_GROUPS[si]
+            se = e - sg[0]
+            nc.scalar.copy(out=y_sb[si][:, :, se * U : (se + 1) * U], in_=y_bank[:])
+            if e == sg[-1]:
+                nc.sync.dma_start(
+                    out=out.rearrange("n (r c) -> n r c", r=R)[:, :, sg[0] * U : (sg[-1] + 1) * U],
+                    in_=y_sb[si][:],
+                )
+
+        gather_words(0, 0)
+        gather_scales(0)
+        gather_words(1, 0)
+        gather_scales(1)
+        gather_words(0, 1)
+        for e in range(EARLY):
+            round_w2(e, nc.scalar.copy, w2_stage[e][:])
+        for e in range(EARLY):
+            w2_mx[e] = quantise(w2_stage[e][:], N, held, "w2_%d" % e)
+
+        for e in range(E):
+            for o in range(PASSES):
+                round_w1(e, o, 0, nc.vector.tensor_copy, w1_stage(e, o, 0)[:])
+                round_w1(e, o, 1, nc.scalar.copy, w1_stage(e, o, 1)[:])
+                if o == 1:
+                    quantise_w1(e, 0, 1)
+                elif e > 0:
+                    quantise_w1(e - 1, 1, 1)
+                quantise_w1(e, o, 0)
+                if o == 0:
+                    if e >= 1:
+                        first_product(e - 1)
+                    if e >= 2:
+                        quantise_h(e - 2)
+                        if e - 2 < EARLY:
+                            second_product(e - 2)
+                    if e + 1 < E:
+                        gather_words(e + 1, 1)
+                else:
+                    if e >= 1:
+                        activate(e - 1)
+                    if e + 2 < E:
+                        gather_words(e + 2, 0)
+                        gather_scales(e + 2)
+
+        quantise_w1(E - 1, 1, 1)
+        first_product(E - 1)
+        activate(E - 1)
+        late = list(range(EARLY, E))
+        late_stage = [stage[(2 * PASSES * E - 2 + i) % 3][:, 0 : N * PACK] for i in range(len(late))]
+        round_w2(late[0], nc.vector.tensor_copy, late_stage[0])
+        for i, e in enumerate(late):
+            if i + 1 < len(late):
+                round_w2(late[i + 1], nc.vector.tensor_copy, late_stage[i + 1])
+            if e >= E - 2:
+                quantise_h(e)
+            w2_mx[e] = quantise(late_stage[i], N, held, "w2_%d" % e)
+            second_product(e)

@@ -23,31 +23,34 @@ U = C // R
 LIST_COLS = C // 16
 
 EARLY = 3
-SETS = 3
 STORE_GROUPS = [(0, 1, 2), (3, 4), (5, 6), (7,)]
+RAW_BYTES = PACK * H * 4
 
 
 def tile_moe_pke_mlp_gelu_kernel(tc, x_words, x_scales, w1, w2, offs, out):
     nc = tc.nc
     with ExitStack() as ctx:
         held = ctx.enter_context(tc.tile_pool(name="held", bufs=1))
-        ring = ctx.enter_context(tc.tile_pool(name="ring", bufs=8))
-        psum_a = ctx.enter_context(tc.psum_pool(name="psum_a", bufs=4))
-        psum_y = ctx.enter_context(tc.psum_pool(name="psum_y", bufs=4))
+        arena = ctx.enter_context(tc.tile_pool(name="arena", bufs=1))
+        ring = ctx.enter_context(tc.tile_pool(name="ring", bufs=12))
+        psum_a = ctx.enter_context(tc.psum_pool(name="psum_a", bufs=6))
+        psum_y = ctx.enter_context(tc.psum_pool(name="psum_y", bufs=2))
+
+        def after_pass(n, place, shape, dtype, name):
+            if n < 0:
+                return held.tile(shape, dtype, name=name, align_bytes=64)
+            return arena.tile(shape, dtype, name=name, align_bytes=64, offset=n * RAW_BYTES + place)
 
         offsets = held.tile([P, E * LIST_COLS], U16, name="offsets")
         tok_words = [held.tile([P, T], I32, name="tok_words%d" % o, align_bytes=64) for o in range(PASSES)]
         tok_scales = held.tile([P, T], U8, name="tok_scales", align_bytes=64)
-        w1_raw = [[held.tile([P, PACK, H], F32, name="w1_raw%d_%d" % (e, o), align_bytes=64) for o in range(PASSES)] for e in range(E)]
+        w1_raw = [[after_pass(PASSES * e + o, 0, [P, PACK, H], F32, "w1_raw%d_%d" % (e, o)) for o in range(PASSES)] for e in range(E)]
         w2_early = held.tile([P, EARLY, PACK, N], F32, name="w2_early", align_bytes=64)
         w2_raw = [w2_early[:, e, :, :] for e in range(EARLY)]
         w2_raw += [held.tile([P, PACK, N], F32, name="w2_late%d" % e, align_bytes=64)[:] for e in range(EARLY, E)]
         y_sb = [held.tile([P, R, len(g) * U], F32, name="y_sb%d" % g[0], align_bytes=64) for g in STORE_GROUPS]
         stage = [held.tile([P, 2 * P * PACK], BF16, name="stage%d" % i, align_bytes=64) for i in range(3)]
-        h_stage = [held.tile([P, C * PACK], BF16, name="h_stage%d" % i, align_bytes=64) for i in range(2)]
         w2_stage = [held.tile([P, N * PACK], BF16, name="w2_stage%d" % e, align_bytes=64) for e in range(EARLY)]
-        slot_words = [[held.tile([P, C], U32, name="slot_words%d_%d" % (s, o), align_bytes=64) for o in range(PASSES)] for s in range(SETS)]
-        slot_scales = [held.tile([P, C], U8, name="slot_scales%d" % s, align_bytes=64) for s in range(SETS)]
         warm_in = held.tile([P, 1], F32, name="warm_in")
         warm_out = held.tile([P, 1], F32, name="warm_out")
 
@@ -79,9 +82,7 @@ def tile_moe_pke_mlp_gelu_kernel(tc, x_words, x_scales, w1, w2, offs, out):
         for e in range(EARLY, E):
             nc.sync.dma_start(out=w2_raw[e], in_=w2[e].rearrange("(p j) n -> p j n", j=PACK))
 
-        def quantise(src, width, pool, name):
-            codes = pool.tile([P, width], U32, name=name + "_codes", align_bytes=64)
-            scales = pool.tile([P, width], U8, name=name + "_scales", align_bytes=64)
+        def quantise(src, codes, scales):
             nc.vector.quantize_mx(out=codes[:].bitcast(FP8X4), scales=scales[:], in_=src)
             return codes, scales
 
@@ -91,31 +92,44 @@ def tile_moe_pke_mlp_gelu_kernel(tc, x_words, x_scales, w1, w2, offs, out):
                 in_=w2_raw[e].rearrange("p j (c i) -> p c j i", i=4),
             )
 
-        def round_w1(e, o, pair, copy, dst):
+        def round_w1(e, o, pair, copy):
             src = w1_raw[e][o][:].rearrange("p j (m t) -> p m j t", t=PACK)[:, :, :, 2 * pair : 2 * pair + 2]
-            copy(out=dst.rearrange("p (t m j) -> p m j t", t=2, j=PACK), in_=src)
+            copy(out=w1_stage(e, o, pair)[:].rearrange("p (t m j) -> p m j t", t=2, j=PACK), in_=src)
 
+        slot_words = {}
+        slot_scales = {}
         w1_mx = {}
         w2_mx = {}
+        h_bf = {}
         h_mx = {}
         banks = {}
 
         def gather_words(e, o):
             cols = slice(e * LIST_COLS, (e + 1) * LIST_COLS)
-            nc.vector.tensor_copy(out=slot_words[e % SETS][o][:], in_=tok_words[o][:].bitcast(U32).indirect(offsets[:, cols]))
+            words = after_pass(PASSES * e + o - 3, 0, [P, C], U32, "slot_words%d_%d" % (e, o))
+            nc.vector.tensor_copy(out=words[:], in_=tok_words[o][:].bitcast(U32).indirect(offsets[:, cols]))
+            slot_words[(e, o)] = words
 
         def gather_scales(e):
             cols = slice(e * LIST_COLS, (e + 1) * LIST_COLS)
-            nc.vector.tensor_copy(out=slot_scales[e % SETS][:], in_=tok_scales[:].indirect(offsets[:, cols]))
+            scales = after_pass(PASSES * e - 3, 1024, [P, C], U8, "slot_scales%d" % e)
+            nc.vector.tensor_copy(out=scales[:], in_=tok_scales[:].indirect(offsets[:, cols]))
+            slot_scales[e] = scales
 
         def w1_stage(e, o, pair):
             return stage[(2 * (PASSES * e + o) + pair) % 3]
 
         def quantise_w1(e, o, pair):
-            w1_mx[(e, o, pair)] = quantise(w1_stage(e, o, pair)[:], 2 * P, ring, "w1")
+            codes = ring.tile([P, 2 * P], U32, name="w1_codes", align_bytes=64)
+            scales = ring.tile([P, 2 * P], U8, name="w1_scales", align_bytes=64)
+            w1_mx[(e, o, pair)] = quantise(w1_stage(e, o, pair)[:], codes, scales)
+
+        def quantise_w2(e, src):
+            codes = held.tile([P, N], U32, name="w2_codes%d" % e, align_bytes=64)
+            scales = held.tile([P, N], U8, name="w2_scales%d" % e, align_bytes=64)
+            w2_mx[e] = quantise(src, codes, scales)
 
         def first_product(e):
-            words, scales = slot_words[e % SETS], slot_scales[e % SETS]
             banks[e] = [psum_a.tile([P, PACK, U], F32, name="a_bank") for r in range(R)]
             for pair in range(2):
                 for r in range(R):
@@ -128,23 +142,28 @@ def tile_moe_pke_mlp_gelu_kernel(tc, x_words, x_scales, w1, w2, offs, out):
                                 out=banks[e][r][:, t, :],
                                 lhsT=wc[:, mcols].bitcast(FP8X4),
                                 lhsT_scale=ws[:, mcols],
-                                rhs=words[o][:, ncols].bitcast(FP8X4),
-                                rhs_scale=scales[4 * o : P, ncols],
+                                rhs=slot_words[(e, o)][:, ncols].bitcast(FP8X4),
+                                rhs_scale=slot_scales[e][4 * o : P, ncols],
                                 start=(o == 0),
                                 stop=(o == PASSES - 1),
                             )
 
         def activate(e):
-            h_bf = h_stage[e % 2]
+            n = PASSES * (e + 1) + 1
+            h_bf[e] = after_pass(n if n < PASSES * E else -1, 2048, [P, C * PACK], BF16, "h_bf%d" % e)
             for r in range(R):
                 nc.scalar.activation(
-                    out=h_bf[:, r * U * PACK : (r + 1) * U * PACK].rearrange("p (u t) -> p u t", t=PACK),
+                    out=h_bf[e][:, r * U * PACK : (r + 1) * U * PACK].rearrange("p (u t) -> p u t", t=PACK),
                     in_=banks[e][r][:].rearrange("p t u -> p u t"),
                     func=GELU,
                 )
 
         def quantise_h(e):
-            h_mx[e] = quantise(h_stage[e % 2][:], C, held, "h%d" % e)
+            n = PASSES * (e + 2)
+            n = n if n < PASSES * E else -1
+            codes = after_pass(n, 2048, [P, C], U32, "h_codes%d" % e)
+            scales = after_pass(n, 3072, [P, C], U8, "h_scales%d" % e)
+            h_mx[e] = quantise(h_bf[e][:], codes, scales)
 
         def second_product(e):
             y_bank = psum_y.tile([P, R, U], F32, name="y_bank")
@@ -175,12 +194,12 @@ def tile_moe_pke_mlp_gelu_kernel(tc, x_words, x_scales, w1, w2, offs, out):
         for e in range(EARLY):
             round_w2(e, nc.scalar.copy, w2_stage[e][:])
         for e in range(EARLY):
-            w2_mx[e] = quantise(w2_stage[e][:], N, held, "w2_%d" % e)
+            quantise_w2(e, w2_stage[e][:])
 
         for e in range(E):
             for o in range(PASSES):
-                round_w1(e, o, 0, nc.vector.tensor_copy, w1_stage(e, o, 0)[:])
-                round_w1(e, o, 1, nc.scalar.copy, w1_stage(e, o, 1)[:])
+                round_w1(e, o, 0, nc.vector.tensor_copy)
+                round_w1(e, o, 1, nc.scalar.copy)
                 if o == 1:
                     quantise_w1(e, 0, 1)
                 elif e > 0:
@@ -206,12 +225,12 @@ def tile_moe_pke_mlp_gelu_kernel(tc, x_words, x_scales, w1, w2, offs, out):
         first_product(E - 1)
         activate(E - 1)
         late = list(range(EARLY, E))
-        late_stage = [stage[(2 * PASSES * E - 2 + i) % 3][:, 0 : N * PACK] for i in range(len(late))]
+        late_stage = [stage[(2 * PASSES * E - 2 + i % 2) % 3][:, (i // 2 % 2) * N * PACK : (i // 2 % 2 + 1) * N * PACK] for i in range(len(late))]
         round_w2(late[0], nc.vector.tensor_copy, late_stage[0])
         for i, e in enumerate(late):
             if i + 1 < len(late):
                 round_w2(late[i + 1], nc.vector.tensor_copy, late_stage[i + 1])
             if e >= E - 2:
                 quantise_h(e)
-            w2_mx[e] = quantise(late_stage[i], N, held, "w2_%d" % e)
+            quantise_w2(e, late_stage[i])
             second_product(e)

@@ -22,9 +22,13 @@ PASSES = K // K_PASS
 U = C // R
 LIST_COLS = C // 16
 
-EARLY = 3
-STORE_GROUPS = [(0, 1, 2), (3, 4), (5, 6), (7,)]
+EARLY = 2
+OUT_GROUPS = [(0, 1), (2, 3), (4, 5), (6,), (7,)]
+SPLIT = (1, 5, 9, 14, 15)
+GATHERS_AFTER = {-1: 5, 1: 1, 3: 2, 5: 1, 7: 2, 9: 1}
+LATE_ON_SCALAR = 0
 RAW_BYTES = PACK * H * 4
+LAST = PASSES * E - 1
 
 
 def tile_moe_pke_mlp_gelu_kernel(tc, x_words, x_scales, w1, w2, offs, out):
@@ -32,9 +36,9 @@ def tile_moe_pke_mlp_gelu_kernel(tc, x_words, x_scales, w1, w2, offs, out):
     with ExitStack() as ctx:
         held = ctx.enter_context(tc.tile_pool(name="held", bufs=1))
         arena = ctx.enter_context(tc.tile_pool(name="arena", bufs=1))
-        ring = ctx.enter_context(tc.tile_pool(name="ring", bufs=12))
-        psum_a = ctx.enter_context(tc.psum_pool(name="psum_a", bufs=6))
-        psum_y = ctx.enter_context(tc.psum_pool(name="psum_y", bufs=2))
+        ring = ctx.enter_context(tc.tile_pool(name="ring", bufs=6))
+        psum_a = ctx.enter_context(tc.psum_pool(name="psum_a", bufs=4))
+        psum_y = ctx.enter_context(tc.psum_pool(name="psum_y", bufs=4))
 
         def after_pass(n, place, shape, dtype, name):
             if n < 0:
@@ -44,13 +48,11 @@ def tile_moe_pke_mlp_gelu_kernel(tc, x_words, x_scales, w1, w2, offs, out):
         offsets = held.tile([P, E * LIST_COLS], U16, name="offsets")
         tok_words = [held.tile([P, T], I32, name="tok_words%d" % o, align_bytes=64) for o in range(PASSES)]
         tok_scales = held.tile([P, T], U8, name="tok_scales", align_bytes=64)
-        w1_raw = [[after_pass(PASSES * e + o, 0, [P, PACK, H], F32, "w1_raw%d_%d" % (e, o)) for o in range(PASSES)] for e in range(E)]
+        w1_raw = [after_pass(n, 0, [P, PACK, H], F32, "w1_raw%d" % n) for n in range(LAST + 1)]
         w2_early = held.tile([P, EARLY, PACK, N], F32, name="w2_early", align_bytes=64)
         w2_raw = [w2_early[:, e, :, :] for e in range(EARLY)]
         w2_raw += [held.tile([P, PACK, N], F32, name="w2_late%d" % e, align_bytes=64)[:] for e in range(EARLY, E)]
-        y_sb = [held.tile([P, R, len(g) * U], F32, name="y_sb%d" % g[0], align_bytes=64) for g in STORE_GROUPS]
-        stage = [held.tile([P, 2 * P * PACK], BF16, name="stage%d" % i, align_bytes=64) for i in range(3)]
-        w2_stage = [held.tile([P, N * PACK], BF16, name="w2_stage%d" % e, align_bytes=64) for e in range(EARLY)]
+        w2_stage = after_pass(-1, 2048, [P, EARLY, N * PACK], BF16, "w2_stage")
         warm_in = held.tile([P, 1], F32, name="warm_in")
         warm_out = held.tile([P, 1], F32, name="warm_out")
 
@@ -61,6 +63,12 @@ def tile_moe_pke_mlp_gelu_kernel(tc, x_words, x_scales, w1, w2, offs, out):
         def load_words(o):
             nc.sync.dma_start(out=tok_words[o][:], in_=x_words[o].rearrange("p n r -> p (n r)").bitcast(I32))
 
+        def load_w2_early():
+            nc.sync.dma_start(
+                out=w2_early[:].rearrange("p e j n -> p e (j n)"),
+                in_=w2[0:EARLY].rearrange("e (p j) n -> p e (j n)", j=PACK),
+            )
+
         nc.sync.dma_start(offsets[:], offs)
         load_words(0)
         for q in range(4):
@@ -68,23 +76,31 @@ def tile_moe_pke_mlp_gelu_kernel(tc, x_words, x_scales, w1, w2, offs, out):
                 out=tok_scales[32 * q : 32 * q + 4 * PASSES, :].bitcast(I32),
                 in_=x_scales[:, 4 * q : 4 * q + 4, :].bitcast(I32),
             )
-        nc.sync.dma_start(
-            out=w2_early[:].rearrange("p e j n -> p e (j n)"),
-            in_=w2[0:EARLY].rearrange("e (p j) n -> p e (j n)", j=PACK),
-        )
-        load_words(1)
-        for e in range(E):
-            for o in range(PASSES):
-                nc.sync.dma_start(
-                    out=w1_raw[e][o][:],
-                    in_=w1[e, o * K_PASS : (o + 1) * K_PASS, :].rearrange("(p j) c -> p j c", j=PACK),
-                )
+        for n in range(LAST + 1):
+            if n == 0:
+                load_w2_early()
+            if n == 0:
+                load_words(1)
+            e, o = divmod(n, PASSES)
+            nc.sync.dma_start(
+                out=w1_raw[n][:],
+                in_=w1[e, o * K_PASS : (o + 1) * K_PASS, :].rearrange("(p j) c -> p j c", j=PACK),
+            )
         for e in range(EARLY, E):
             nc.sync.dma_start(out=w2_raw[e], in_=w2[e].rearrange("(p j) n -> p j n", j=PACK))
 
+        stage = {}
+        slot_words = {}
+        slot_scales = {}
+        w1_mx = {}
+        w2_mx = {}
+        h_bf = {}
+        h_mx = {}
+        a_banks = {}
+        y_banks = {}
+
         def quantise(src, codes, scales):
-            nc.vector.quantize_mx(out=codes[:].bitcast(FP8X4), scales=scales[:], in_=src)
-            return codes, scales
+            nc.vector.quantize_mx(out=codes.bitcast(FP8X4), scales=scales, in_=src)
 
         def round_w2(e, copy, dst):
             copy(
@@ -92,145 +108,165 @@ def tile_moe_pke_mlp_gelu_kernel(tc, x_words, x_scales, w1, w2, offs, out):
                 in_=w2_raw[e].rearrange("p j (c i) -> p c j i", i=4),
             )
 
-        def round_w1(e, o, pair, copy):
-            src = w1_raw[e][o][:].rearrange("p j (m t) -> p m j t", t=PACK)[:, :, :, 2 * pair : 2 * pair + 2]
-            copy(out=w1_stage(e, o, pair)[:].rearrange("p (t m j) -> p m j t", t=2, j=PACK), in_=src)
+        def round_w1(n):
+            src = w1_raw[n][:].rearrange("p j (m t) -> p m j t", t=PACK)
+            if n in SPLIT:
+                stage[n] = [ring.tile([P, 2, P * PACK], BF16, name="half_stage", align_bytes=64, bufs=4)[:] for half in range(2)]
+                copies = (nc.vector.tensor_copy, nc.scalar.copy)
+            else:
+                whole = ring.tile([P, PACK, P * PACK], BF16, name="stage", align_bytes=64, bufs=3)
+                stage[n] = [whole[:, 0:2, :], whole[:, 2:4, :], whole[:]]
+                copies = (nc.vector.tensor_copy,) * 2 if n % 2 else (nc.scalar.copy,) * 2
+            for half in range(2):
+                copies[half](out=stage[n][half].rearrange("p t (m j) -> p m j t", j=PACK), in_=src[:, :, :, 2 * half : 2 * half + 2])
 
-        slot_words = {}
-        slot_scales = {}
-        w1_mx = {}
-        w2_mx = {}
-        h_bf = {}
-        h_mx = {}
-        banks = {}
+        def gather_step(k, n):
+            g, step = divmod(k, 3)
+            cols = slice(2 * g * LIST_COLS, 2 * (g + 1) * LIST_COLS)
+            if step == 1:
+                slot_scales[g] = after_pass(n, 4096 + k % 2 * 2048, [P, 2 * C], U8, "slot_scales%d" % g)
+                nc.vector.tensor_copy(out=slot_scales[g][:], in_=tok_scales[:].indirect(offsets[:, cols]))
+            else:
+                o = step // 2
+                slot_words[(g, o)] = after_pass(n, 4096 + k % 2 * 2048, [P, 2 * C], U32, "slot_words%d_%d" % (g, o))
+                nc.vector.tensor_copy(out=slot_words[(g, o)][:], in_=tok_words[o][:].bitcast(U32).indirect(offsets[:, cols]))
 
-        def gather_words(e, o):
-            cols = slice(e * LIST_COLS, (e + 1) * LIST_COLS)
-            words = after_pass(PASSES * e + o - 3, 0, [P, C], U32, "slot_words%d_%d" % (e, o))
-            nc.vector.tensor_copy(out=words[:], in_=tok_words[o][:].bitcast(U32).indirect(offsets[:, cols]))
-            slot_words[(e, o)] = words
+        def quantise_w1(n):
+            for first, count in ((0, 2), (2, 2)) if n in SPLIT else ((0, PACK),):
+                codes = ring.tile([P, count * P], U32, name="w1_codes", align_bytes=64)
+                scales = ring.tile([P, count * P], U8, name="w1_scales", align_bytes=64)
+                src = stage[n][first // 2 if count == 2 else 2]
+                quantise(src.rearrange("p t c -> p (t c)"), codes[:], scales[:])
+                for t in range(count):
+                    w1_mx[(n, first + t)] = (codes[:, t * P : (t + 1) * P], scales[:, t * P : (t + 1) * P])
 
-        def gather_scales(e):
-            cols = slice(e * LIST_COLS, (e + 1) * LIST_COLS)
-            scales = after_pass(PASSES * e - 3, 1024, [P, C], U8, "slot_scales%d" % e)
-            nc.vector.tensor_copy(out=scales[:], in_=tok_scales[:].indirect(offsets[:, cols]))
-            slot_scales[e] = scales
-
-        def w1_stage(e, o, pair):
-            return stage[(2 * (PASSES * e + o) + pair) % 3]
-
-        def quantise_w1(e, o, pair):
-            codes = ring.tile([P, 2 * P], U32, name="w1_codes", align_bytes=64)
-            scales = ring.tile([P, 2 * P], U8, name="w1_scales", align_bytes=64)
-            w1_mx[(e, o, pair)] = quantise(w1_stage(e, o, pair)[:], codes, scales)
-
-        def quantise_w2(e, src):
-            codes = held.tile([P, N], U32, name="w2_codes%d" % e, align_bytes=64)
-            scales = held.tile([P, N], U8, name="w2_scales%d" % e, align_bytes=64)
-            w2_mx[e] = quantise(src, codes, scales)
+        def quantise_w2(first, count, src):
+            codes = held.tile([P, count * N], U32, name="w2_codes%d" % first, align_bytes=64)
+            scales = held.tile([P, count * N], U8, name="w2_scales%d" % first, align_bytes=64)
+            quantise(src, codes[:], scales[:])
+            for i in range(count):
+                w2_mx[first + i] = (codes[:, i * N : (i + 1) * N], scales[:, i * N : (i + 1) * N])
 
         def first_product(e):
-            banks[e] = [psum_a.tile([P, PACK, U], F32, name="a_bank") for r in range(R)]
-            for pair in range(2):
+            a_banks[e] = [psum_a.tile([P, PACK, U], F32, name="a_bank") for r in range(R)]
+            for ts in (((0, 1), (2, 3)) if e == E - 1 else ((0, 1, 2, 3),)):
                 for r in range(R):
-                    ncols = slice(r * U, (r + 1) * U)
-                    for t in (2 * pair, 2 * pair + 1):
-                        mcols = slice((t % 2) * P, (t % 2 + 1) * P)
+                    ncols = slice((e % 2) * C + r * U, (e % 2) * C + (r + 1) * U)
+                    for t in ts:
                         for o in range(PASSES):
-                            wc, ws = w1_mx[(e, o, pair)]
+                            wc, ws = w1_mx[(PASSES * e + o, t)]
                             nc.tensor.matmul_mx(
-                                out=banks[e][r][:, t, :],
-                                lhsT=wc[:, mcols].bitcast(FP8X4),
-                                lhsT_scale=ws[:, mcols],
-                                rhs=slot_words[(e, o)][:, ncols].bitcast(FP8X4),
-                                rhs_scale=slot_scales[e][4 * o : P, ncols],
+                                out=a_banks[e][r][:, t, :],
+                                lhsT=wc.bitcast(FP8X4),
+                                lhsT_scale=ws,
+                                rhs=slot_words[(e // 2, o)][:, ncols].bitcast(FP8X4),
+                                rhs_scale=slot_scales[e // 2][4 * o : P, ncols],
                                 start=(o == 0),
                                 stop=(o == PASSES - 1),
                             )
 
         def activate(e):
-            n = PASSES * (e + 1) + 1
-            h_bf[e] = after_pass(n if n < PASSES * E else -1, 2048, [P, C * PACK], BF16, "h_bf%d" % e)
+            n = (PASSES * (e + 1) if e < E - 2 else LAST) if e < E - 1 else LAST + 2
+            h_bf[e] = after_pass(n, 2048, [P, R, U * PACK], BF16, "h_bf%d" % e)
             for r in range(R):
                 nc.scalar.activation(
-                    out=h_bf[e][:, r * U * PACK : (r + 1) * U * PACK].rearrange("p (u t) -> p u t", t=PACK),
-                    in_=banks[e][r][:].rearrange("p t u -> p u t"),
+                    out=h_bf[e][:, r, :].rearrange("p (u t) -> p u t", t=PACK),
+                    in_=a_banks[e][r][:].rearrange("p t u -> p u t"),
                     func=GELU,
                 )
 
-        def quantise_h(e):
-            n = PASSES * (e + 2)
-            n = n if n < PASSES * E else -1
-            codes = after_pass(n, 2048, [P, C], U32, "h_codes%d" % e)
-            scales = after_pass(n, 3072, [P, C], U8, "h_scales%d" % e)
-            h_mx[e] = quantise(h_bf[e][:], codes, scales)
+        def quantise_h(e, ranks):
+            if e not in h_mx:
+                n = -1
+                h_mx[e] = (after_pass(n, 0, [P, C], U32, "h_codes%d" % e), after_pass(n, 1024, [P, C], U8, "h_scales%d" % e))
+            cols = slice(ranks.start * U, ranks.stop * U)
+            quantise(h_bf[e][:, ranks, :].rearrange("p r c -> p (r c)"), h_mx[e][0][:, cols], h_mx[e][1][:, cols])
 
-        def second_product(e):
-            y_bank = psum_y.tile([P, R, U], F32, name="y_bank")
+        def group_of(e):
+            return [g for g in OUT_GROUPS if e in g][0]
+
+        def second_product(e, ranks):
+            g = group_of(e)
+            if (g, ranks.start) not in y_banks:
+                y_banks[(g, ranks.start)] = psum_y.tile([P, len(g), ranks.stop - ranks.start, U], F32, name="y_bank")
+            cols = slice(ranks.start * U, ranks.stop * U)
             nc.tensor.matmul_mx(
-                out=y_bank[:].rearrange("p r u -> p (r u)"),
-                lhsT=w2_mx[e][0][:].bitcast(FP8X4),
-                lhsT_scale=w2_mx[e][1][:],
-                rhs=h_mx[e][0][:].bitcast(FP8X4),
-                rhs_scale=h_mx[e][1][:],
+                out=y_banks[(g, ranks.start)][:, e - g[0], :, :].rearrange("p r u -> p (r u)"),
+                lhsT=w2_mx[e][0].bitcast(FP8X4),
+                lhsT_scale=w2_mx[e][1],
+                rhs=h_mx[e][0][:, cols].bitcast(FP8X4),
+                rhs_scale=h_mx[e][1][:, cols],
                 start=True,
                 stop=True,
             )
-            si = [i for i, g in enumerate(STORE_GROUPS) if e in g][0]
-            sg = STORE_GROUPS[si]
-            se = e - sg[0]
-            nc.scalar.copy(out=y_sb[si][:, :, se * U : (se + 1) * U], in_=y_bank[:])
-            if e == sg[-1]:
-                nc.sync.dma_start(
-                    out=out.rearrange("n (r c) -> n r c", r=R)[:, :, sg[0] * U : (sg[-1] + 1) * U],
-                    in_=y_sb[si][:],
-                )
 
-        gather_words(0, 0)
-        gather_scales(0)
-        gather_words(1, 0)
-        gather_scales(1)
-        gather_words(0, 1)
-        for e in range(EARLY):
-            round_w2(e, nc.scalar.copy, w2_stage[e][:])
-        for e in range(EARLY):
-            quantise_w2(e, w2_stage[e][:])
+        def put_out(g, ranks, copy, n, place=2048):
+            y_sb = after_pass(n, place, [P, ranks.stop - ranks.start, len(g), U], F32, "y_sb%d_%d" % (g[0], ranks.start))
+            copy(out=y_sb[:], in_=y_banks[(g, ranks.start)][:].rearrange("p e r u -> p r e u"))
+            nc.sync.dma_start(
+                out=out.rearrange("n (r c) -> n r c", r=R)[:, ranks, g[0] * U : (g[-1] + 1) * U],
+                in_=y_sb[:].rearrange("p r e u -> p r (e u)"),
+            )
 
-        for e in range(E):
-            for o in range(PASSES):
-                round_w1(e, o, 0, nc.vector.tensor_copy)
-                round_w1(e, o, 1, nc.scalar.copy)
-                if o == 1:
-                    quantise_w1(e, 0, 1)
-                elif e > 0:
-                    quantise_w1(e - 1, 1, 1)
-                quantise_w1(e, o, 0)
-                if o == 0:
-                    if e >= 1:
-                        first_product(e - 1)
-                    if e >= 2:
-                        quantise_h(e - 2)
-                        if e - 2 < EARLY:
-                            second_product(e - 2)
-                    if e + 1 < E:
-                        gather_words(e + 1, 1)
-                else:
-                    if e >= 1:
-                        activate(e - 1)
-                    if e + 2 < E:
-                        gather_words(e + 2, 0)
-                        gather_scales(e + 2)
+        both = slice(0, R)
 
-        quantise_w1(E - 1, 1, 1)
-        first_product(E - 1)
-        activate(E - 1)
+        def early_w2():
+            for e in range(EARLY):
+                round_w2(e, nc.scalar.copy, w2_stage[:, e, :])
+            for first, count in ((0, 2),):
+                quantise_w2(first, count, w2_stage[:, first : first + count, :].rearrange("p e c -> p (e c)"))
+
+        gathered = 0
+        for k in range(GATHERS_AFTER[-1]):
+            gather_step(k, -1)
+        gathered = GATHERS_AFTER[-1]
+        early_w2()
+        for n in range(LAST + 1):
+            e, o = divmod(n, PASSES)
+            round_w1(n)
+            if o == 0 and 1 <= e < E - 1:
+                activate(e - 1)
+            if o == 1 and 1 <= e < E - 1:
+                quantise_h(e - 1, both)
+                if e - 1 < EARLY:
+                    second_product(e - 1, both)
+            quantise_w1(n)
+            if o == 1:
+                first_product(e)
+            if o == 0 and 0 <= e - 2 < EARLY and group_of(e - 2)[-1] == e - 2:
+                put_out(group_of(e - 2), both, nc.scalar.copy, n, 0)
+            for k in range(gathered, gathered + GATHERS_AFTER.get(n, 0)):
+                gather_step(k, n)
+            gathered += GATHERS_AFTER.get(n, 0)
+
+        activate(E - 2)
         late = list(range(EARLY, E))
-        late_stage = [stage[(2 * PASSES * E - 2 + i % 2) % 3][:, (i // 2 % 2) * N * PACK : (i // 2 % 2 + 1) * N * PACK] for i in range(len(late))]
-        round_w2(late[0], nc.vector.tensor_copy, late_stage[0])
+        late_stage = {}
         for i, e in enumerate(late):
-            if i + 1 < len(late):
-                round_w2(late[i + 1], nc.vector.tensor_copy, late_stage[i + 1])
-            if e >= E - 2:
-                quantise_h(e)
-            quantise_w2(e, late_stage[i])
-            second_product(e)
+            if i < LATE_ON_SCALAR:
+                late_stage[e] = after_pass(LAST, i * 1024, [P, N * PACK], BF16, "late_stage%d" % e)[:]
+                round_w2(e, nc.scalar.copy, late_stage[e])
+            else:
+                late_stage[e] = stage[LAST][1][:, i % 2, :]
+        activate(E - 1)
+        for i, e in enumerate(late):
+            for ahead in range(i if i == 0 else i + 1, min(i + 2, len(late))):
+                if ahead >= LATE_ON_SCALAR:
+                    round_w2(late[ahead], nc.vector.tensor_copy, late_stage[late[ahead]])
+            if e == E - 2:
+                quantise_h(E - 2, both)
+            quantise_w2(e, 1, late_stage[e])
+            if e < E - 1:
+                second_product(e, both)
+        halves = [slice(r, r + 1) for r in range(R)]
+        for ranks in halves:
+            quantise_h(E - 1, ranks)
+            second_product(E - 1, ranks)
+        for g in OUT_GROUPS[:-1]:
+            if g[-1] >= EARLY:
+                if g[0] in (6,):
+                    put_out(g, both, nc.vector.tensor_copy, LAST + 2)
+                else:
+                    put_out(g, both, nc.scalar.copy, -1)
+        for ranks in halves:
+            put_out(OUT_GROUPS[-1], ranks, nc.scalar.copy, -1)

@@ -14,6 +14,8 @@ U16 = mybir.dt.uint16
 U8 = mybir.dt.uint8
 FP8X4 = mybir.dt.float8_e4m3fn_x4
 GELU = mybir.ActivationFunctionType.Gelu_apprx_tanh
+WIDTH = {"f32": 4, "bf16": 2, "u32": 4, "u8": 1}
+DTYPE = {"f32": F32, "bf16": BF16, "u32": U32, "u8": U8}
 
 P = 128
 PACK = 4
@@ -21,14 +23,17 @@ K_PASS = P * PACK
 PASSES = K // K_PASS
 U = C // R
 LIST_COLS = C // 16
+LAST = PASSES * E - 1
 
 EARLY = 2
+SCALAR_ALONE = 6
+SCALAR_EVERY = 2
+SCALAR_PHASE = 1
+LAST_SPLIT = 3
+W2_ON_SCALAR = (2, 3, 4)
+W2_LOADS = [(0, 1), (2,), (3,), (4,), (5, 6), (7,)]
 OUT_GROUPS = [(0, 1), (2, 3), (4, 5), (6,), (7,)]
-SPLIT = (1, 5, 9, 14, 15)
-GATHERS_AFTER = {-1: 5, 1: 1, 3: 2, 5: 1, 7: 2, 9: 1}
-LATE_ON_SCALAR = 0
-RAW_BYTES = PACK * H * 4
-LAST = PASSES * E - 1
+OUT_ON_VECTOR = (4,)
 
 
 def tile_moe_pke_mlp_gelu_kernel(tc, x_words, x_scales, w1, w2, offs, out):
@@ -36,63 +41,80 @@ def tile_moe_pke_mlp_gelu_kernel(tc, x_words, x_scales, w1, w2, offs, out):
     with ExitStack() as ctx:
         held = ctx.enter_context(tc.tile_pool(name="held", bufs=1))
         arena = ctx.enter_context(tc.tile_pool(name="arena", bufs=1))
-        ring = ctx.enter_context(tc.tile_pool(name="ring", bufs=6))
-        psum_a = ctx.enter_context(tc.psum_pool(name="psum_a", bufs=4))
-        psum_y = ctx.enter_context(tc.psum_pool(name="psum_y", bufs=4))
+        psum = ctx.enter_context(tc.psum_pool(name="psum", bufs=8))
 
-        def after_pass(n, place, shape, dtype, name):
-            if n < 0:
-                return held.tile(shape, dtype, name=name, align_bytes=64)
-            return arena.tile(shape, dtype, name=name, align_bytes=64, offset=n * RAW_BYTES + place)
+        spans = {"fresh": [0, 0]}
+
+        def place(name, shape, kind, on="fresh", room=0):
+            size = WIDTH[kind]
+            for d in shape[1:]:
+                size = size * d
+            size = max((size + 63) // 64 * 64, room)
+            if isinstance(on, list):
+                on = [x for x in on if x == "fresh" or spans[x][0] + size <= spans[x][1]][0]
+            at = spans[on][0]
+            spans[on][0] = at + size
+            assert on == "fresh" or spans[on][0] <= spans[on][1], name
+            spans[name] = [at, at + size]
+            return arena.tile(shape, DTYPE[kind], name=name, align_bytes=64, offset=at)
 
         offsets = held.tile([P, E * LIST_COLS], U16, name="offsets")
         tok_words = [held.tile([P, T], I32, name="tok_words%d" % o, align_bytes=64) for o in range(PASSES)]
         tok_scales = held.tile([P, T], U8, name="tok_scales", align_bytes=64)
-        w1_raw = [after_pass(n, 0, [P, PACK, H], F32, "w1_raw%d" % n) for n in range(LAST + 1)]
-        w2_early = held.tile([P, EARLY, PACK, N], F32, name="w2_early", align_bytes=64)
-        w2_raw = [w2_early[:, e, :, :] for e in range(EARLY)]
-        w2_raw += [held.tile([P, PACK, N], F32, name="w2_late%d" % e, align_bytes=64)[:] for e in range(EARLY, E)]
-        w2_stage = after_pass(-1, 2048, [P, EARLY, N * PACK], BF16, "w2_stage")
-        warm_in = held.tile([P, 1], F32, name="warm_in")
-        warm_out = held.tile([P, 1], F32, name="warm_out")
+        zero = held.tile([P, 1], F32, name="zero")
+        bias = held.tile([P, 1], F32, name="bias")
+        w1_raw = [place("w1_raw%d" % n, [P, PACK, H], "f32") for n in range(LAST + 1)]
+        w2_raw = {}
+        for g in W2_LOADS:
+            both = place("w2_raw%d" % g[0], [P, len(g), PACK, N], "f32")
+            for i, e in enumerate(g):
+                w2_raw[e] = (both, i)
 
-        nc.vector.memset(warm_in[:], 0.0)
-        nc.scalar.activation(out=warm_out[:], in_=warm_in[:], func=GELU)
         nc.vector.memset(tok_scales[:].bitcast(I32), 0)
+        nc.vector.memset(zero[:], 0.0)
+        nc.scalar.activation(out=bias[:], in_=zero[:], func=GELU)
 
         def load_words(o):
             nc.sync.dma_start(out=tok_words[o][:], in_=x_words[o].rearrange("p n r -> p (n r)").bitcast(I32))
 
-        def load_w2_early():
-            nc.sync.dma_start(
-                out=w2_early[:].rearrange("p e j n -> p e (j n)"),
-                in_=w2[0:EARLY].rearrange("e (p j) n -> p e (j n)", j=PACK),
-            )
+        def load_scales():
+            for q in range(4):
+                nc.sync.dma_start(
+                    out=tok_scales[32 * q : 32 * q + 4 * PASSES, :].bitcast(I32),
+                    in_=x_scales[:, 4 * q : 4 * q + 4, :].bitcast(I32),
+                )
 
-        nc.sync.dma_start(offsets[:], offs)
-        load_words(0)
-        for q in range(4):
-            nc.sync.dma_start(
-                out=tok_scales[32 * q : 32 * q + 4 * PASSES, :].bitcast(I32),
-                in_=x_scales[:, 4 * q : 4 * q + 4, :].bitcast(I32),
-            )
-        for n in range(LAST + 1):
-            if n == 0:
-                load_w2_early()
-            if n == 0:
-                load_words(1)
+        def load_w1(n):
             e, o = divmod(n, PASSES)
             nc.sync.dma_start(
                 out=w1_raw[n][:],
                 in_=w1[e, o * K_PASS : (o + 1) * K_PASS, :].rearrange("(p j) c -> p j c", j=PACK),
             )
-        for e in range(EARLY, E):
-            nc.sync.dma_start(out=w2_raw[e], in_=w2[e].rearrange("(p j) n -> p j n", j=PACK))
+
+        def load_w2(g):
+            nc.sync.dma_start(
+                out=w2_raw[g[0]][0][:].rearrange("p e j n -> p e (j n)"),
+                in_=w2[g[0] : g[-1] + 1].rearrange("e (p j) n -> p e (j n)", j=PACK),
+            )
+
+        nc.sync.dma_start(offsets[:], offs)
+        load_words(0)
+        for n in range(LAST + 1):
+            load_w1(n)
+            if n == 1:
+                load_scales()
+            if n == 3:
+                load_words(1)
+            if n == 10 and EARLY:
+                load_w2(W2_LOADS[0])
+        for g in W2_LOADS[1 if EARLY else 0 :]:
+            load_w2(g)
 
         stage = {}
         slot_words = {}
         slot_scales = {}
         w1_mx = {}
+        w2_stage = {}
         w2_mx = {}
         h_bf = {}
         h_mx = {}
@@ -102,85 +124,80 @@ def tile_moe_pke_mlp_gelu_kernel(tc, x_words, x_scales, w1, w2, offs, out):
         def quantise(src, codes, scales):
             nc.vector.quantize_mx(out=codes.bitcast(FP8X4), scales=scales, in_=src)
 
-        def round_w2(e, copy, dst):
+        def on_scalar(n):
+            return n < SCALAR_ALONE or (n < LAST and n % SCALAR_EVERY == SCALAR_PHASE)
+
+        def gather_words(g, o, on="fresh"):
+            cols = slice(2 * g * LIST_COLS, 2 * (g + 1) * LIST_COLS)
+            slot_words[(g, o)] = place("slot_words%d_%d" % (g, o), [P, 2 * C], "u32", on)
+            nc.vector.tensor_copy(out=slot_words[(g, o)][:], in_=tok_words[o][:].bitcast(U32).indirect(offsets[:, cols]))
+
+        def gather_scales(g):
+            cols = slice(2 * g * LIST_COLS, 2 * (g + 1) * LIST_COLS)
+            slot_scales[g] = place("slot_scales%d" % g, [P, 2 * C], "u8")
+            nc.vector.tensor_copy(out=slot_scales[g][:], in_=tok_scales[:].indirect(offsets[:, cols]))
+
+        def round_w1(n, copy, ts, on):
+            name = "stage%d_%d" % (n, ts.start)
+            tile = place(name, [P, ts.stop - ts.start, P * PACK], "bf16", on)
+            stage[(n, ts.start)] = (tile, ts)
+            src = w1_raw[n][:].rearrange("p j (m t) -> p m j t", t=PACK)
+            copy(out=tile[:].rearrange("p t (m j) -> p m j t", j=PACK), in_=src[:, :, :, ts])
+
+        def quantise_w1(n, first, on="fresh"):
+            tile, ts = stage[(n, first)]
+            count = ts.stop - ts.start
+            codes = place("w1_codes%d_%d" % (n, first), [P, count * P], "u32", on)
+            scales = place("w1_scales%d_%d" % (n, first), [P, count * P], "u8", on)
+            quantise(tile[:].rearrange("p t c -> p (t c)"), codes[:], scales[:])
+            for t in range(count):
+                w1_mx[(n, first + t)] = (codes[:, t * P : (t + 1) * P], scales[:, t * P : (t + 1) * P])
+
+        def round_w2(e, copy, on):
+            w2_stage[e] = place("w2_stage%d" % e, [P, N * PACK], "bf16", on, 2048)
             copy(
-                out=dst.rearrange("p (c i j) -> p c j i", i=4, j=PACK),
-                in_=w2_raw[e].rearrange("p j (c i) -> p c j i", i=4),
+                out=w2_stage[e][:].rearrange("p (c i j) -> p c j i", i=4, j=PACK),
+                in_=w2_raw[e][0][:, w2_raw[e][1], :, :].rearrange("p j (c i) -> p c j i", i=4),
             )
 
-        def round_w1(n):
-            src = w1_raw[n][:].rearrange("p j (m t) -> p m j t", t=PACK)
-            if n in SPLIT:
-                stage[n] = [ring.tile([P, 2, P * PACK], BF16, name="half_stage", align_bytes=64, bufs=4)[:] for half in range(2)]
-                copies = (nc.vector.tensor_copy, nc.scalar.copy)
-            else:
-                whole = ring.tile([P, PACK, P * PACK], BF16, name="stage", align_bytes=64, bufs=3)
-                stage[n] = [whole[:, 0:2, :], whole[:, 2:4, :], whole[:]]
-                copies = (nc.vector.tensor_copy,) * 2 if n % 2 else (nc.scalar.copy,) * 2
-            for half in range(2):
-                copies[half](out=stage[n][half].rearrange("p t (m j) -> p m j t", j=PACK), in_=src[:, :, :, 2 * half : 2 * half + 2])
+        def quantise_w2(e, on="fresh"):
+            codes = place("w2_codes%d" % e, [P, N], "u32", on)
+            scales = place("w2_scales%d" % e, [P, N], "u8", on)
+            quantise(w2_stage[e][:], codes[:], scales[:])
+            w2_mx[e] = (codes[:], scales[:])
 
-        def gather_step(k, n):
-            g, step = divmod(k, 3)
-            cols = slice(2 * g * LIST_COLS, 2 * (g + 1) * LIST_COLS)
-            if step == 1:
-                slot_scales[g] = after_pass(n, 4096 + k % 2 * 2048, [P, 2 * C], U8, "slot_scales%d" % g)
-                nc.vector.tensor_copy(out=slot_scales[g][:], in_=tok_scales[:].indirect(offsets[:, cols]))
-            else:
-                o = step // 2
-                slot_words[(g, o)] = after_pass(n, 4096 + k % 2 * 2048, [P, 2 * C], U32, "slot_words%d_%d" % (g, o))
-                nc.vector.tensor_copy(out=slot_words[(g, o)][:], in_=tok_words[o][:].bitcast(U32).indirect(offsets[:, cols]))
+        def first_product(e, r):
+            a_banks[(e, r)] = psum.tile([P, PACK, U], F32, name="bank")
+            ncols = slice((e % 2) * C + r * U, (e % 2) * C + (r + 1) * U)
+            for t in range(PACK):
+                for o in range(PASSES):
+                    wc, ws = w1_mx[(PASSES * e + o, t)]
+                    nc.tensor.matmul_mx(
+                        out=a_banks[(e, r)][:, t, :],
+                        lhsT=wc.bitcast(FP8X4),
+                        lhsT_scale=ws,
+                        rhs=slot_words[(e // 2, o)][:, ncols].bitcast(FP8X4),
+                        rhs_scale=slot_scales[e // 2][4 * o : P, ncols],
+                        start=(o == 0),
+                        stop=(o == PASSES - 1),
+                    )
 
-        def quantise_w1(n):
-            for first, count in ((0, 2), (2, 2)) if n in SPLIT else ((0, PACK),):
-                codes = ring.tile([P, count * P], U32, name="w1_codes", align_bytes=64)
-                scales = ring.tile([P, count * P], U8, name="w1_scales", align_bytes=64)
-                src = stage[n][first // 2 if count == 2 else 2]
-                quantise(src.rearrange("p t c -> p (t c)"), codes[:], scales[:])
-                for t in range(count):
-                    w1_mx[(n, first + t)] = (codes[:, t * P : (t + 1) * P], scales[:, t * P : (t + 1) * P])
+        def activate(e, r, on):
+            h_bf[(e, r)] = place("h_bf%d_%d" % (e, r), [P, U * PACK], "bf16", on)
+            nc.scalar.activation(
+                out=h_bf[(e, r)][:].rearrange("p (u t) -> p u t", t=PACK),
+                in_=a_banks[(e, r)][:].rearrange("p t u -> p u t"),
+                func=GELU,
+                bias=bias[:],
+            )
 
-        def quantise_w2(first, count, src):
-            codes = held.tile([P, count * N], U32, name="w2_codes%d" % first, align_bytes=64)
-            scales = held.tile([P, count * N], U8, name="w2_scales%d" % first, align_bytes=64)
-            quantise(src, codes[:], scales[:])
-            for i in range(count):
-                w2_mx[first + i] = (codes[:, i * N : (i + 1) * N], scales[:, i * N : (i + 1) * N])
-
-        def first_product(e):
-            a_banks[e] = [psum_a.tile([P, PACK, U], F32, name="a_bank") for r in range(R)]
-            for ts in (((0, 1), (2, 3)) if e == E - 1 else ((0, 1, 2, 3),)):
-                for r in range(R):
-                    ncols = slice((e % 2) * C + r * U, (e % 2) * C + (r + 1) * U)
-                    for t in ts:
-                        for o in range(PASSES):
-                            wc, ws = w1_mx[(PASSES * e + o, t)]
-                            nc.tensor.matmul_mx(
-                                out=a_banks[e][r][:, t, :],
-                                lhsT=wc.bitcast(FP8X4),
-                                lhsT_scale=ws,
-                                rhs=slot_words[(e // 2, o)][:, ncols].bitcast(FP8X4),
-                                rhs_scale=slot_scales[e // 2][4 * o : P, ncols],
-                                start=(o == 0),
-                                stop=(o == PASSES - 1),
-                            )
-
-        def activate(e):
-            n = (PASSES * (e + 1) if e < E - 2 else LAST) if e < E - 1 else LAST + 2
-            h_bf[e] = after_pass(n, 2048, [P, R, U * PACK], BF16, "h_bf%d" % e)
-            for r in range(R):
-                nc.scalar.activation(
-                    out=h_bf[e][:, r, :].rearrange("p (u t) -> p u t", t=PACK),
-                    in_=a_banks[e][r][:].rearrange("p t u -> p u t"),
-                    func=GELU,
-                )
-
-        def quantise_h(e, ranks):
-            if e not in h_mx:
-                n = -1
-                h_mx[e] = (after_pass(n, 0, [P, C], U32, "h_codes%d" % e), after_pass(n, 1024, [P, C], U8, "h_scales%d" % e))
-            cols = slice(ranks.start * U, ranks.stop * U)
-            quantise(h_bf[e][:, ranks, :].rearrange("p r c -> p (r c)"), h_mx[e][0][:, cols], h_mx[e][1][:, cols])
+        def quantise_h(e, r, on="fresh"):
+            key = (e, r) if e == E - 1 else (e, 0)
+            width = U if e == E - 1 else C
+            if key not in h_mx:
+                h_mx[key] = (place("h_codes%d_%d" % key, [P, width], "u32", on), place("h_scales%d_%d" % key, [P, width], "u8", on))
+            cols = slice(0, U) if e == E - 1 else slice(r * U, (r + 1) * U)
+            quantise(h_bf[(e, r)][:], h_mx[key][0][:, cols], h_mx[key][1][:, cols])
 
         def group_of(e):
             return [g for g in OUT_GROUPS if e in g][0]
@@ -188,20 +205,20 @@ def tile_moe_pke_mlp_gelu_kernel(tc, x_words, x_scales, w1, w2, offs, out):
         def second_product(e, ranks):
             g = group_of(e)
             if (g, ranks.start) not in y_banks:
-                y_banks[(g, ranks.start)] = psum_y.tile([P, len(g), ranks.stop - ranks.start, U], F32, name="y_bank")
-            cols = slice(ranks.start * U, ranks.stop * U)
+                y_banks[(g, ranks.start)] = psum.tile([P, len(g), ranks.stop - ranks.start, U], F32, name="bank")
+            key = (e, ranks.start)
             nc.tensor.matmul_mx(
                 out=y_banks[(g, ranks.start)][:, e - g[0], :, :].rearrange("p r u -> p (r u)"),
                 lhsT=w2_mx[e][0].bitcast(FP8X4),
                 lhsT_scale=w2_mx[e][1],
-                rhs=h_mx[e][0][:, cols].bitcast(FP8X4),
-                rhs_scale=h_mx[e][1][:, cols],
+                rhs=h_mx[key][0][:].bitcast(FP8X4),
+                rhs_scale=h_mx[key][1][:],
                 start=True,
                 stop=True,
             )
 
-        def put_out(g, ranks, copy, n, place=2048):
-            y_sb = after_pass(n, place, [P, ranks.stop - ranks.start, len(g), U], F32, "y_sb%d_%d" % (g[0], ranks.start))
+        def put_out(g, ranks, copy, on):
+            y_sb = place("y_sb%d_%d" % (g[0], ranks.start), [P, ranks.stop - ranks.start, len(g), U], "f32", on)
             copy(out=y_sb[:], in_=y_banks[(g, ranks.start)][:].rearrange("p e r u -> p r e u"))
             nc.sync.dma_start(
                 out=out.rearrange("n (r c) -> n r c", r=R)[:, ranks, g[0] * U : (g[-1] + 1) * U],
@@ -209,64 +226,119 @@ def tile_moe_pke_mlp_gelu_kernel(tc, x_words, x_scales, w1, w2, offs, out):
             )
 
         both = slice(0, R)
+        halves = [slice(r, r + 1) for r in range(R)]
+        whole = slice(0, PACK)
 
-        def early_w2():
-            for e in range(EARLY):
-                round_w2(e, nc.scalar.copy, w2_stage[:, e, :])
-            for first, count in ((0, 2),):
-                quantise_w2(first, count, w2_stage[:, first : first + count, :].rearrange("p e c -> p (e c)"))
+        def old(n):
+            return ["w1_raw%d" % m for m in range(n - 3)] + ["fresh"]
 
-        gathered = 0
-        for k in range(GATHERS_AFTER[-1]):
-            gather_step(k, -1)
-        gathered = GATHERS_AFTER[-1]
-        early_w2()
-        for n in range(LAST + 1):
-            e, o = divmod(n, PASSES)
-            round_w1(n)
-            if o == 0 and 1 <= e < E - 1:
-                activate(e - 1)
-            if o == 1 and 1 <= e < E - 1:
-                quantise_h(e - 1, both)
-                if e - 1 < EARLY:
-                    second_product(e - 1, both)
-            quantise_w1(n)
-            if o == 1:
-                first_product(e)
-            if o == 0 and 0 <= e - 2 < EARLY and group_of(e - 2)[-1] == e - 2:
-                put_out(group_of(e - 2), both, nc.scalar.copy, n, 0)
-            for k in range(gathered, gathered + GATHERS_AFTER.get(n, 0)):
-                gather_step(k, n)
-            gathered += GATHERS_AFTER.get(n, 0)
+        def raw(n):
+            return "w1_raw%d" % n if n >= 0 else "fresh"
 
-        activate(E - 2)
-        late = list(range(EARLY, E))
-        late_stage = {}
-        for i, e in enumerate(late):
-            if i < LATE_ON_SCALAR:
-                late_stage[e] = after_pass(LAST, i * 1024, [P, N * PACK], BF16, "late_stage%d" % e)[:]
-                round_w2(e, nc.scalar.copy, late_stage[e])
-            else:
-                late_stage[e] = stage[LAST][1][:, i % 2, :]
-        activate(E - 1)
-        for i, e in enumerate(late):
-            for ahead in range(i if i == 0 else i + 1, min(i + 2, len(late))):
-                if ahead >= LATE_ON_SCALAR:
-                    round_w2(late[ahead], nc.vector.tensor_copy, late_stage[late[ahead]])
-            if e == E - 2:
-                quantise_h(E - 2, both)
-            quantise_w2(e, 1, late_stage[e])
+        def round_halves(n, copies):
+            for half in range(2):
+                round_w1(n, copies[half], slice(2 * half, 2 * half + 2), old(n))
+
+        def quantise_halves(n):
+            for first in (0, 2):
+                quantise_w1(n, first, old(n))
+
+        def products(e):
+            for r in range(R):
+                first_product(e, r)
+
+        def gelu(e, on):
+            for r in range(R):
+                activate(e, r, on)
+
+        on_vector = (nc.vector.tensor_copy, nc.vector.tensor_copy)
+        for g in range(E // 2):
+            gather_words(g, 0)
+        for g in range(E // 2):
+            gather_scales(g)
+        def finish(e):
+            second_product(e, both)
+            if group_of(e)[-1] == e:
+                g = group_of(e)
+                put_out(g, both, nc.vector.tensor_copy if g[0] in OUT_ON_VECTOR else nc.scalar.copy, old(LAST))
+
+        def quantise_h_both(e, on):
+            for r in range(R):
+                quantise_h(e, r, on)
+
+        for n in range(4):
+            round_w1(n, nc.scalar.copy, whole, "fresh")
+        quantise_w1(0, 0)
+        quantise_w1(1, 0, raw(2))
+        quantise_w1(2, 0)
+        for g in range(E // 2):
+            gather_words(g, 1)
+        products(0)
+        quantise_w1(3, 0)
+        products(1)
+        round_w1(4, nc.scalar.copy, whole, old(4))
+        quantise_w1(4, 0)
+        round_w1(5, nc.scalar.copy, whole, old(5))
+        gelu(0, raw(5))
+        gelu(1, raw(5))
+
+        def vector_pass(n):
+            round_halves(n, on_vector)
+            quantise_w1(n, 0, old(n))
+            if (n - 1, 0) not in w1_mx:
+                quantise_w1(n - 1, 0, raw(n))
+            quantise_w1(n, 2, old(n))
+
+        vector_pass(6)
+        products(2)
+        gelu(2, old(6))
+        quantise_h_both(0, "stage6_0")
+        quantise_h_both(1, "stage6_2")
+        vector_pass(7)
+        products(3)
+        for e in range(4, E - 1):
+            n = PASSES * e
+            round_w1(n, nc.scalar.copy, whole, old(n))
+            gelu(e - 1, old(n))
+            if e == 5:
+                for early in range(EARLY):
+                    round_w2(early, nc.vector.tensor_copy, old(n))
+                for early in range(EARLY):
+                    quantise_w2(early)
+                    finish(early)
+            vector_pass(n + 1)
+            products(e)
+            if e == 4:
+                quantise_h_both(2, "stage%d_0" % (n + 1))
+            quantise_h_both(e - 1, "stage%d_2" % (n + 1) if e == 4 else "stage%d_0" % (n + 1))
+        round_halves(LAST - 1, (nc.vector.tensor_copy, nc.scalar.copy))
+        quantise_halves(LAST - 1)
+        gelu(E - 2, old(LAST))
+        vector_pass(LAST)
+        products(E - 1)
+        for e in W2_ON_SCALAR:
+            round_w2(e, nc.scalar.copy, old(LAST))
+        quantise_w2(EARLY)
+        quantise_h_both(E - 2, "stage%d_0" % LAST)
+        quantise_w2(EARLY + 1)
+        gelu(E - 1, "w2_raw%d" % W2_ON_SCALAR[-1])
+        for e in range(EARLY, EARLY + 2):
+            second_product(e, both)
+        late = [e for e in range(EARLY, E) if e not in W2_ON_SCALAR]
+        round_w2(late.pop(0), nc.vector.tensor_copy, old(LAST))
+        for e in range(EARLY + 2, E):
+            if late and e != EARLY + 3:
+                round_w2(late.pop(0), nc.vector.tensor_copy, old(LAST))
+            if e == E - 1:
+                quantise_h(E - 1, 0)
+            quantise_w2(e, "fresh")
             if e < E - 1:
                 second_product(e, both)
-        halves = [slice(r, r + 1) for r in range(R)]
+        put_out(OUT_GROUPS[1], both, nc.scalar.copy, old(LAST))
+        quantise_h(E - 1, 1, "w2_stage%d" % (E - 1))
         for ranks in halves:
-            quantise_h(E - 1, ranks)
             second_product(E - 1, ranks)
-        for g in OUT_GROUPS[:-1]:
-            if g[-1] >= EARLY:
-                if g[0] in (6,):
-                    put_out(g, both, nc.vector.tensor_copy, LAST + 2)
-                else:
-                    put_out(g, both, nc.scalar.copy, -1)
-        for ranks in halves:
-            put_out(OUT_GROUPS[-1], ranks, nc.scalar.copy, -1)
+        for g in OUT_GROUPS[2:-1]:
+            put_out(g, both, nc.vector.tensor_copy if g[0] in OUT_ON_VECTOR else nc.scalar.copy, "w2_stage%d" % (E - 2) if g[0] in OUT_ON_VECTOR else old(LAST))
+        put_out(OUT_GROUPS[-1], halves[0], nc.scalar.copy, old(LAST))
+        put_out(OUT_GROUPS[-1], halves[1], nc.vector.tensor_copy, old(LAST))

@@ -26,14 +26,9 @@ LIST_COLS = C // 16
 LAST = PASSES * E - 1
 
 EARLY = 2
-SCALAR_ALONE = 6
-SCALAR_EVERY = 2
-SCALAR_PHASE = 1
-LAST_SPLIT = 3
-W2_ON_SCALAR = (2, 3, 4)
+W2_ON_SCALAR = (3, 4)
 W2_LOADS = [(0, 1), (2,), (3,), (4,), (5, 6), (7,)]
-OUT_GROUPS = [(0, 1), (2, 3), (4, 5), (6,), (7,)]
-OUT_ON_VECTOR = (4,)
+OUT_GROUPS = [(0, 1), (2, 3), (4, 5), (6, 7)]
 
 
 def tile_moe_pke_mlp_gelu_kernel(tc, x_words, x_scales, w1, w2, offs, out):
@@ -105,9 +100,9 @@ def tile_moe_pke_mlp_gelu_kernel(tc, x_words, x_scales, w1, w2, offs, out):
                 load_scales()
             if n == 3:
                 load_words(1)
-            if n == 10 and EARLY:
+            if n == 13:
                 load_w2(W2_LOADS[0])
-        for g in W2_LOADS[1 if EARLY else 0 :]:
+        for g in W2_LOADS[1:]:
             load_w2(g)
 
         stage = {}
@@ -120,12 +115,11 @@ def tile_moe_pke_mlp_gelu_kernel(tc, x_words, x_scales, w1, w2, offs, out):
         h_mx = {}
         a_banks = {}
         y_banks = {}
+        y_of = {}
+        y_sb = {}
 
         def quantise(src, codes, scales):
             nc.vector.quantize_mx(out=codes.bitcast(FP8X4), scales=scales, in_=src)
-
-        def on_scalar(n):
-            return n < SCALAR_ALONE or (n < LAST and n % SCALAR_EVERY == SCALAR_PHASE)
 
         def gather_words(g, o, on="fresh"):
             cols = slice(2 * g * LIST_COLS, 2 * (g + 1) * LIST_COLS)
@@ -192,38 +186,39 @@ def tile_moe_pke_mlp_gelu_kernel(tc, x_words, x_scales, w1, w2, offs, out):
             )
 
         def quantise_h(e, r, on="fresh"):
-            key = (e, r) if e == E - 1 else (e, 0)
-            width = U if e == E - 1 else C
-            if key not in h_mx:
-                h_mx[key] = (place("h_codes%d_%d" % key, [P, width], "u32", on), place("h_scales%d_%d" % key, [P, width], "u8", on))
-            cols = slice(0, U) if e == E - 1 else slice(r * U, (r + 1) * U)
-            quantise(h_bf[(e, r)][:], h_mx[key][0][:, cols], h_mx[key][1][:, cols])
+            if e not in h_mx:
+                h_mx[e] = (place("h_codes%d" % e, [P, C], "u32", on), place("h_scales%d" % e, [P, C], "u8", on))
+            cols = slice(r * U, (r + 1) * U)
+            quantise(h_bf[(e, r)][:], h_mx[e][0][:, cols], h_mx[e][1][:, cols])
 
-        def group_of(e):
-            return [g for g in OUT_GROUPS if e in g][0]
-
-        def second_product(e, ranks):
-            g = group_of(e)
-            if (g, ranks.start) not in y_banks:
-                y_banks[(g, ranks.start)] = psum.tile([P, len(g), ranks.stop - ranks.start, U], F32, name="bank")
-            key = (e, ranks.start)
+        def second_product(e):
+            pair = e // 2
+            if pair not in y_banks or e == E - 1:
+                y_banks[pair] = psum.tile([P, 2, R, U], F32, name="bank")
+            y_of[e] = y_banks[pair]
             nc.tensor.matmul_mx(
-                out=y_banks[(g, ranks.start)][:, e - g[0], :, :].rearrange("p r u -> p (r u)"),
+                out=y_of[e][:, e % 2, :, :].rearrange("p r u -> p (r u)"),
                 lhsT=w2_mx[e][0].bitcast(FP8X4),
                 lhsT_scale=w2_mx[e][1],
-                rhs=h_mx[key][0][:].bitcast(FP8X4),
-                rhs_scale=h_mx[key][1][:],
+                rhs=h_mx[e][0][:].bitcast(FP8X4),
+                rhs_scale=h_mx[e][1][:],
                 start=True,
                 stop=True,
             )
 
-        def put_out(g, ranks, copy, on):
-            y_sb = place("y_sb%d_%d" % (g[0], ranks.start), [P, ranks.stop - ranks.start, len(g), U], "f32", on)
-            copy(out=y_sb[:], in_=y_banks[(g, ranks.start)][:].rearrange("p e r u -> p r e u"))
-            nc.sync.dma_start(
-                out=out.rearrange("n (r c) -> n r c", r=R)[:, ranks, g[0] * U : (g[-1] + 1) * U],
-                in_=y_sb[:].rearrange("p r e u -> p r (e u)"),
+        def copy_out(first, count, copy, on):
+            g = [g for g in OUT_GROUPS if first in g][0]
+            if g not in y_sb:
+                y_sb[g] = place("y_sb%d" % g[0], [P, R, len(g), U], "f32", on)
+            copy(
+                out=y_sb[g][:, :, first - g[0] : first - g[0] + count, :],
+                in_=y_of[first][:, first % 2 : first % 2 + count].rearrange("p e r u -> p r e u"),
             )
+            if first + count - 1 == g[-1]:
+                nc.sync.dma_start(
+                    out=out.rearrange("n (r c) -> n r c", r=R)[:, :, g[0] * U : (g[-1] + 1) * U],
+                    in_=y_sb[g][:].rearrange("p r e u -> p r (e u)"),
+                )
 
         both = slice(0, R)
         halves = [slice(r, r + 1) for r in range(R)]
@@ -252,20 +247,22 @@ def tile_moe_pke_mlp_gelu_kernel(tc, x_words, x_scales, w1, w2, offs, out):
                 activate(e, r, on)
 
         on_vector = (nc.vector.tensor_copy, nc.vector.tensor_copy)
-        for g in range(E // 2):
-            gather_words(g, 0)
-        for g in range(E // 2):
-            gather_scales(g)
-        def finish(e):
-            second_product(e, both)
-            if group_of(e)[-1] == e:
-                g = group_of(e)
-                put_out(g, both, nc.vector.tensor_copy if g[0] in OUT_ON_VECTOR else nc.scalar.copy, old(LAST))
 
         def quantise_h_both(e, on):
             for r in range(R):
                 quantise_h(e, r, on)
 
+        def vector_pass(n):
+            round_halves(n, on_vector)
+            quantise_w1(n, 0, old(n))
+            if (n - 1, 0) not in w1_mx:
+                quantise_w1(n - 1, 0, raw(n))
+            quantise_w1(n, 2, old(n))
+
+        for g in range(E // 2):
+            gather_words(g, 0)
+        for g in range(E // 2):
+            gather_scales(g)
         for n in range(4):
             round_w1(n, nc.scalar.copy, whole, "fresh")
         quantise_w1(0, 0)
@@ -282,13 +279,6 @@ def tile_moe_pke_mlp_gelu_kernel(tc, x_words, x_scales, w1, w2, offs, out):
         gelu(0, raw(5))
         gelu(1, raw(5))
 
-        def vector_pass(n):
-            round_halves(n, on_vector)
-            quantise_w1(n, 0, old(n))
-            if (n - 1, 0) not in w1_mx:
-                quantise_w1(n - 1, 0, raw(n))
-            quantise_w1(n, 2, old(n))
-
         vector_pass(6)
         products(2)
         gelu(2, old(6))
@@ -298,47 +288,65 @@ def tile_moe_pke_mlp_gelu_kernel(tc, x_words, x_scales, w1, w2, offs, out):
         products(3)
         for e in range(4, E - 1):
             n = PASSES * e
-            round_w1(n, nc.scalar.copy, whole, old(n))
+            if e < E - 2:
+                round_w1(n, nc.scalar.copy, whole, old(n))
+            else:
+                round_halves(n, (nc.vector.tensor_copy, nc.scalar.copy))
+                quantise_halves(n)
             gelu(e - 1, old(n))
-            if e == 5:
-                for early in range(EARLY):
-                    round_w2(early, nc.vector.tensor_copy, old(n))
-                for early in range(EARLY):
-                    quantise_w2(early)
-                    finish(early)
             vector_pass(n + 1)
             products(e)
             if e == 4:
                 quantise_h_both(2, "stage%d_0" % (n + 1))
             quantise_h_both(e - 1, "stage%d_2" % (n + 1) if e == 4 else "stage%d_0" % (n + 1))
-        round_halves(LAST - 1, (nc.vector.tensor_copy, nc.scalar.copy))
-        quantise_halves(LAST - 1)
+        for e in range(EARLY):
+            round_w2(e, nc.scalar.copy, old(LAST))
         gelu(E - 2, old(LAST))
-        vector_pass(LAST)
+        for e in range(EARLY):
+            quantise_w2(e)
+            second_product(e)
+        copy_out(0, 2, nc.scalar.copy, old(LAST))
+        vector_pass(LAST - 1)
+        spare = psum.tile([P, 2 * C], F32, name="bank")
+        for repeat in range(2):
+            wc, ws = w1_mx[(LAST - 1, PACK - 1)]
+            nc.tensor.matmul_mx(
+                out=spare[:],
+                lhsT=wc.bitcast(FP8X4),
+                lhsT_scale=ws,
+                rhs=slot_words[(E // 2 - 1, 0)][:].bitcast(FP8X4),
+                rhs_scale=slot_scales[E // 2 - 1][:],
+                start=True,
+                stop=True,
+            )
+        quantise_h_both(E - 2, "stage%d_0" % (LAST - 1))
+
+        def finish(e):
+            quantise_w2(e)
+            second_product(e)
+
+        round_halves(LAST, (nc.vector.tensor_copy, nc.scalar.copy))
+        round_w2(2, nc.vector.tensor_copy, old(LAST))
+        quantise_w1(LAST, 0, old(LAST))
+        quantise_w2(2)
+        quantise_w1(LAST, 2, old(LAST))
         products(E - 1)
+        second_product(2)
         for e in W2_ON_SCALAR:
             round_w2(e, nc.scalar.copy, old(LAST))
-        quantise_w2(EARLY)
-        quantise_h_both(E - 2, "stage%d_0" % LAST)
-        quantise_w2(EARLY + 1)
-        gelu(E - 1, "w2_raw%d" % W2_ON_SCALAR[-1])
-        for e in range(EARLY, EARLY + 2):
-            second_product(e, both)
-        late = [e for e in range(EARLY, E) if e not in W2_ON_SCALAR]
-        round_w2(late.pop(0), nc.vector.tensor_copy, old(LAST))
-        for e in range(EARLY + 2, E):
-            if late and e != EARLY + 3:
-                round_w2(late.pop(0), nc.vector.tensor_copy, old(LAST))
-            if e == E - 1:
-                quantise_h(E - 1, 0)
-            quantise_w2(e, "fresh")
-            if e < E - 1:
-                second_product(e, both)
-        put_out(OUT_GROUPS[1], both, nc.scalar.copy, old(LAST))
-        quantise_h(E - 1, 1, "w2_stage%d" % (E - 1))
-        for ranks in halves:
-            second_product(E - 1, ranks)
-        for g in OUT_GROUPS[2:-1]:
-            put_out(g, both, nc.vector.tensor_copy if g[0] in OUT_ON_VECTOR else nc.scalar.copy, "w2_stage%d" % (E - 2) if g[0] in OUT_ON_VECTOR else old(LAST))
-        put_out(OUT_GROUPS[-1], halves[0], nc.scalar.copy, old(LAST))
-        put_out(OUT_GROUPS[-1], halves[1], nc.vector.tensor_copy, old(LAST))
+        activate(E - 1, 0, "w2_raw%d" % W2_ON_SCALAR[-1])
+        finish(3)
+        finish(4)
+        activate(E - 1, 1, "w2_raw%d" % W2_ON_SCALAR[-1])
+        copy_out(2, 2, nc.scalar.copy, old(LAST))
+        round_w2(5, nc.vector.tensor_copy, old(LAST))
+        round_w2(6, nc.vector.tensor_copy, old(LAST))
+        finish(5)
+        copy_out(4, 2, nc.scalar.copy, old(LAST))
+        quantise_h(E - 1, 0, "w2_raw5")
+        round_w2(7, nc.vector.tensor_copy, old(LAST))
+        finish(6)
+        quantise_h(E - 1, 1, "w2_raw5")
+        finish(7)
+        copy_out(6, 1, nc.vector.tensor_copy, "stage%d_2" % LAST)
+        copy_out(7, 1, nc.scalar.copy, old(LAST))

@@ -27,7 +27,7 @@ LAST = PASSES * E - 1
 
 EARLY = 2
 W2_ON_SCALAR = (3, 4)
-W2_LOADS = [(0, 1), (2,), (3,), (4,), (5, 6), (7,)]
+W2_LOADS = [(0, 1), (2,), (3,), (4,), (5,), (6,), (7,)]
 OUT_GROUPS = [(0, 1), (2, 3), (4, 5), (6, 7)]
 
 
@@ -94,10 +94,9 @@ def tile_moe_pke_mlp_gelu_kernel(tc, x_words, x_scales, w1, w2, offs, out):
 
         nc.sync.dma_start(offsets[:], offs)
         load_words(0)
+        load_scales()
         for n in range(LAST + 1):
             load_w1(n)
-            if n == 1:
-                load_scales()
             if n == 3:
                 load_words(1)
             if n == 13:
@@ -266,7 +265,7 @@ def tile_moe_pke_mlp_gelu_kernel(tc, x_words, x_scales, w1, w2, offs, out):
         for n in range(4):
             round_w1(n, nc.scalar.copy, whole, "fresh")
         quantise_w1(0, 0)
-        quantise_w1(1, 0, raw(2))
+        quantise_w1(1, 0)
         quantise_w1(2, 0)
         for g in range(E // 2):
             gather_words(g, 1)
@@ -334,19 +333,18 @@ def tile_moe_pke_mlp_gelu_kernel(tc, x_words, x_scales, w1, w2, offs, out):
         second_product(2)
         for e in W2_ON_SCALAR:
             round_w2(e, nc.scalar.copy, old(LAST))
-        activate(E - 1, 0, "w2_raw%d" % W2_ON_SCALAR[-1])
+        gelu(E - 1, old(LAST))
         finish(3)
-        finish(4)
-        activate(E - 1, 1, "w2_raw%d" % W2_ON_SCALAR[-1])
-        copy_out(2, 2, nc.scalar.copy, old(LAST))
         round_w2(5, nc.vector.tensor_copy, old(LAST))
-        round_w2(6, nc.vector.tensor_copy, old(LAST))
+        finish(4)
+        copy_out(2, 2, nc.scalar.copy, old(LAST))
         finish(5)
         copy_out(4, 2, nc.scalar.copy, old(LAST))
-        quantise_h(E - 1, 0, "w2_raw5")
-        round_w2(7, nc.vector.tensor_copy, old(LAST))
+        round_w2(6, nc.vector.tensor_copy, old(LAST))
+        quantise_h(E - 1, 0, "w2_stage5")
         finish(6)
-        quantise_h(E - 1, 1, "w2_raw5")
+        round_w2(7, nc.vector.tensor_copy, old(LAST))
+        quantise_h(E - 1, 1, old(LAST))
         finish(7)
         copy_out(6, 1, nc.vector.tensor_copy, "stage%d_2" % LAST)
         copy_out(7, 1, nc.scalar.copy, old(LAST))

@@ -25,9 +25,9 @@ U = C // R
 LIST_COLS = C // 16
 LAST = PASSES * E - 1
 
-EARLY = 2
+EARLY = 0
 W2_ON_SCALAR = (3, 4)
-W2_LOADS = [(0, 1), (2,), (3,), (4,), (5,), (6,), (7,)]
+W2_LOADS = [(e,) for e in range(E)]
 OUT_GROUPS = [(0, 1), (2, 3), (4, 5), (6, 7)]
 
 
@@ -99,9 +99,7 @@ def tile_moe_pke_mlp_gelu_kernel(tc, x_words, x_scales, w1, w2, offs, out):
             load_w1(n)
             if n == 3:
                 load_words(1)
-            if n == 13:
-                load_w2(W2_LOADS[0])
-        for g in W2_LOADS[1:]:
+        for g in W2_LOADS:
             load_w2(g)
 
         stage = {}
@@ -298,13 +296,7 @@ def tile_moe_pke_mlp_gelu_kernel(tc, x_words, x_scales, w1, w2, offs, out):
             if e == 4:
                 quantise_h_both(2, "stage%d_0" % (n + 1))
             quantise_h_both(e - 1, "stage%d_2" % (n + 1) if e == 4 else "stage%d_0" % (n + 1))
-        for e in range(EARLY):
-            round_w2(e, nc.scalar.copy, old(LAST))
         gelu(E - 2, old(LAST))
-        for e in range(EARLY):
-            quantise_w2(e)
-            second_product(e)
-        copy_out(0, 2, nc.scalar.copy, old(LAST))
         vector_pass(LAST - 1)
         spare = psum.tile([P, 2 * C], F32, name="bank")
         for repeat in range(2):
@@ -325,26 +317,24 @@ def tile_moe_pke_mlp_gelu_kernel(tc, x_words, x_scales, w1, w2, offs, out):
             second_product(e)
 
         round_halves(LAST, (nc.vector.tensor_copy, nc.scalar.copy))
-        round_w2(2, nc.vector.tensor_copy, old(LAST))
+        round_w2(0, nc.vector.tensor_copy, old(LAST))
         quantise_w1(LAST, 0, old(LAST))
-        quantise_w2(2)
+        finish(0)
         quantise_w1(LAST, 2, old(LAST))
+        round_w2(1, nc.scalar.copy, old(LAST))
+        round_w2(2, nc.vector.tensor_copy, old(LAST))
+        finish(1)
         products(E - 1)
-        second_product(2)
-        for e in W2_ON_SCALAR:
-            round_w2(e, nc.scalar.copy, old(LAST))
-        gelu(E - 1, old(LAST))
-        finish(3)
-        round_w2(5, nc.vector.tensor_copy, old(LAST))
-        finish(4)
-        copy_out(2, 2, nc.scalar.copy, old(LAST))
-        finish(5)
-        copy_out(4, 2, nc.scalar.copy, old(LAST))
-        round_w2(6, nc.vector.tensor_copy, old(LAST))
-        quantise_h(E - 1, 0, "w2_stage5")
-        finish(6)
-        round_w2(7, nc.vector.tensor_copy, old(LAST))
-        quantise_h(E - 1, 1, old(LAST))
-        finish(7)
-        copy_out(6, 1, nc.vector.tensor_copy, "stage%d_2" % LAST)
+        activate(E - 1, 0, old(LAST))
+        copy_out(0, 2, nc.scalar.copy, old(LAST))
+        activate(E - 1, 1, old(LAST))
+        finish(2)
+        for e in range(3, E):
+            round_w2(e, nc.scalar.copy if e == E - 2 else nc.vector.tensor_copy, old(LAST))
+            if e - 4 in range(R):
+                quantise_h(E - 1, e - 4, "w2_stage3")
+            finish(e)
+            if e in (3, 5):
+                copy_out(e - 1, 2, nc.scalar.copy, old(LAST))
+        copy_out(6, 1, nc.vector.tensor_copy, "w2_stage%d" % (E - 1))
         copy_out(7, 1, nc.scalar.copy, old(LAST))

@@ -25,6 +25,7 @@ U = C // R
 LIST_COLS = C // 16
 LAST = PASSES * E - 1
 
+WIDE = 6
 EARLY = 0
 W2_ON_SCALAR = (3, 4)
 W2_LOADS = [(e,) for e in range(E)]
@@ -110,6 +111,7 @@ def tile_moe_pke_mlp_gelu_kernel(tc, x_words, x_scales, w1, w2, offs, out):
         w2_mx = {}
         h_bf = {}
         h_mx = {}
+        h_pairs = {}
         a_banks = {}
         y_banks = {}
         y_of = {}
@@ -156,6 +158,30 @@ def tile_moe_pke_mlp_gelu_kernel(tc, x_words, x_scales, w1, w2, offs, out):
             scales = place("w2_scales%d" % e, [P, N], "u8", on)
             quantise(w2_stage[e][:], codes[:], scales[:])
             w2_mx[e] = (codes[:], scales[:])
+
+        def wide_product(e, a):
+            a_banks[(e, a)] = psum.tile([P, 2, C], F32, name="bank")
+            ncols = slice((e % 2) * C, (e % 2 + 1) * C)
+            for t in range(2):
+                for o in range(PASSES):
+                    wc, ws = w1_mx[(PASSES * e + o, 2 * a + t)]
+                    nc.tensor.matmul_mx(
+                        out=a_banks[(e, a)][:, t, :],
+                        lhsT=wc.bitcast(FP8X4),
+                        lhsT_scale=ws,
+                        rhs=slot_words[(e // 2, o)][:, ncols].bitcast(FP8X4),
+                        rhs_scale=slot_scales[e // 2][4 * o : P, ncols],
+                        start=(o == 0),
+                        stop=(o == PASSES - 1),
+                    )
+
+        def wide_activate(e, a):
+            nc.scalar.activation(
+                out=h_pairs[e][:, a, :].rearrange("p (u t) -> p u t", t=2),
+                in_=a_banks[(e, a)][:].rearrange("p t u -> p u t"),
+                func=GELU,
+                bias=bias[:],
+            )
 
         def first_product(e, r):
             a_banks[(e, r)] = psum.tile([P, PACK, U], F32, name="bank")
@@ -237,15 +263,31 @@ def tile_moe_pke_mlp_gelu_kernel(tc, x_words, x_scales, w1, w2, offs, out):
 
         def products(e):
             for r in range(R):
-                first_product(e, r)
+                if e < WIDE:
+                    wide_product(e, r)
+                else:
+                    first_product(e, r)
 
         def gelu(e, on):
+            if e < WIDE:
+                h_pairs[e] = place("h_pairs%d" % e, [P, 2, C * 2], "bf16", on)
             for r in range(R):
-                activate(e, r, on)
+                if e < WIDE:
+                    wide_activate(e, r)
+                else:
+                    activate(e, r, on)
 
         on_vector = (nc.vector.tensor_copy, nc.vector.tensor_copy)
 
         def quantise_h_both(e, on):
+            if e < WIDE:
+                for r in range(R):
+                    h_bf[(e, r)] = place("h_bf%d_%d" % (e, r), [P, U * PACK], "bf16", on)
+                    nc.vector.tensor_copy(
+                        out=h_bf[(e, r)][:].bitcast(F32).rearrange("p (u a) -> p u a", a=2),
+                        in_=h_pairs[e][:].rearrange("p a c -> p (a c)").bitcast(F32).rearrange("p (a u) -> p u a", a=2)[:, r * U : (r + 1) * U, :],
+                    )
+                on = "fresh"
             for r in range(R):
                 quantise_h(e, r, on)
 

@@ -28,8 +28,8 @@ LAST = PASSES * E - 1
 WIDE = 6
 EARLY = 0
 W2_ON_SCALAR = (3, 4)
-W2_LOADS = [(e,) for e in range(E)]
-OUT_GROUPS = [(0, 1), (2, 3), (4, 5), (6, 7)]
+W2_LOADS = [(0,), (1,), (2,), (3,), (4, 5), (6, 7)]
+OUT_GROUPS = [(0, 1), (2, 3), (4, 5), (6,), (7,)]
 
 
 def tile_moe_pke_mlp_gelu_kernel(tc, x_words, x_scales, w1, w2, offs, out):
@@ -209,10 +209,26 @@ def tile_moe_pke_mlp_gelu_kernel(tc, x_words, x_scales, w1, w2, offs, out):
             )
 
         def quantise_h(e, r, on="fresh"):
-            if e not in h_mx:
-                h_mx[e] = (place("h_codes%d" % e, [P, C], "u32", on), place("h_scales%d" % e, [P, C], "u8", on))
-            cols = slice(r * U, (r + 1) * U)
-            quantise(h_bf[(e, r)][:], h_mx[e][0][:, cols], h_mx[e][1][:, cols])
+            key = (e, r) if e == E - 1 else e
+            width = U if e == E - 1 else C
+            if key not in h_mx:
+                name = "%d_%d" % (e, r)
+                h_mx[key] = (place("h_codes" + name, [P, width], "u32", on), place("h_scales" + name, [P, width], "u8", on))
+            cols = slice(0, U) if e == E - 1 else slice(r * U, (r + 1) * U)
+            quantise(h_bf[(e, r)][:], h_mx[key][0][:, cols], h_mx[key][1][:, cols])
+
+        def last_product(r, copy):
+            bank = psum.tile([P, U], F32, name="bank")
+            nc.tensor.matmul_mx(
+                out=bank[:],
+                lhsT=w2_mx[E - 1][0].bitcast(FP8X4),
+                lhsT_scale=w2_mx[E - 1][1],
+                rhs=h_mx[(E - 1, r)][0][:].bitcast(FP8X4),
+                rhs_scale=h_mx[(E - 1, r)][1][:],
+                start=True,
+                stop=True,
+            )
+            copy(out=y_last[:, r, :], in_=bank[:])
 
         def second_product(e):
             pair = e // 2
@@ -291,6 +307,19 @@ def tile_moe_pke_mlp_gelu_kernel(tc, x_words, x_scales, w1, w2, offs, out):
             for r in range(R):
                 quantise_h(e, r, on)
 
+        def warm_up(stationary):
+            spare = psum.tile([P, 2 * C], F32, name="bank")
+            for repeat in range(2):
+                nc.tensor.matmul_mx(
+                    out=spare[:],
+                    lhsT=stationary[0].bitcast(FP8X4),
+                    lhsT_scale=stationary[1],
+                    rhs=slot_words[(E // 2 - 1, 0)][:].bitcast(FP8X4),
+                    rhs_scale=slot_scales[E // 2 - 1][:],
+                    start=True,
+                    stop=True,
+                )
+
         def vector_pass(n):
             round_halves(n, on_vector)
             quantise_w1(n, 0, old(n))
@@ -340,19 +369,7 @@ def tile_moe_pke_mlp_gelu_kernel(tc, x_words, x_scales, w1, w2, offs, out):
             quantise_h_both(e - 1, "stage%d_2" % (n + 1) if e == 4 else "stage%d_0" % (n + 1))
         gelu(E - 2, old(LAST))
         vector_pass(LAST - 1)
-        spare = psum.tile([P, 2 * C], F32, name="bank")
-        for repeat in range(2):
-            wc, ws = w1_mx[(LAST - 1, PACK - 1)]
-            nc.tensor.matmul_mx(
-                out=spare[:],
-                lhsT=wc.bitcast(FP8X4),
-                lhsT_scale=ws,
-                rhs=slot_words[(E // 2 - 1, 0)][:].bitcast(FP8X4),
-                rhs_scale=slot_scales[E // 2 - 1][:],
-                start=True,
-                stop=True,
-            )
-        quantise_h_both(E - 2, "stage%d_0" % (LAST - 1))
+        warm_up(w1_mx[(LAST - 1, PACK - 1)])
 
         def finish(e):
             quantise_w2(e)
@@ -362,21 +379,32 @@ def tile_moe_pke_mlp_gelu_kernel(tc, x_words, x_scales, w1, w2, offs, out):
         round_w2(0, nc.vector.tensor_copy, old(LAST))
         quantise_w1(LAST, 0, old(LAST))
         finish(0)
+        quantise_h(E - 2, 0, "stage%d_0" % LAST)
         quantise_w1(LAST, 2, old(LAST))
-        round_w2(1, nc.scalar.copy, old(LAST))
-        round_w2(2, nc.vector.tensor_copy, old(LAST))
+        for e in (1, 2):
+            round_w2(e, nc.scalar.copy, old(LAST))
+        quantise_h(E - 2, 1, old(LAST))
         finish(1)
         products(E - 1)
-        activate(E - 1, 0, old(LAST))
+        gelu(E - 1, old(LAST))
         copy_out(0, 2, nc.scalar.copy, old(LAST))
-        activate(E - 1, 1, old(LAST))
+        round_w2(3, nc.vector.tensor_copy, old(LAST))
         finish(2)
-        for e in range(3, E):
-            round_w2(e, nc.scalar.copy if e == E - 2 else nc.vector.tensor_copy, old(LAST))
-            if e - 4 in range(R):
-                quantise_h(E - 1, e - 4, "w2_stage3")
-            finish(e)
-            if e in (3, 5):
-                copy_out(e - 1, 2, nc.scalar.copy, old(LAST))
-        copy_out(6, 1, nc.vector.tensor_copy, "w2_stage%d" % (E - 1))
-        copy_out(7, 1, nc.scalar.copy, old(LAST))
+        finish(3)
+        warm_up(w2_mx[3])
+        copy_out(2, 2, nc.scalar.copy, old(LAST))
+        quantise_h(E - 1, 0, "w2_stage3")
+        for pair in ((4, 5), (6, 7)):
+            for e in pair:
+                round_w2(e, nc.vector.tensor_copy, old(LAST))
+            finish(pair[0])
+            if pair[1] < E - 1:
+                finish(pair[1])
+                quantise_h(E - 1, 1, "w2_stage4")
+        quantise_w2(E - 1)
+        copy_out(4, 2, nc.scalar.copy, old(LAST))
+        copy_out(6, 1, nc.scalar.copy, old(LAST))
+        y_last = place("y_last", [P, R, U], "f32", old(LAST))
+        last_product(0, nc.scalar.copy)
+        last_product(1, nc.vector.tensor_copy)
+        nc.sync.dma_start(out=out.rearrange("n (r c) -> n r c", r=R)[:, :, (E - 1) * U : E * U], in_=y_last[:])

@@ -24,6 +24,7 @@ PASSES = K // K_PASS
 U = C // R
 LIST_COLS = C // 16
 LAST = PASSES * E - 1
+ALIGN = 256
 
 WIDE = 6
 EARLY = 0
@@ -45,18 +46,18 @@ def tile_moe_pke_mlp_gelu_kernel(tc, x_words, x_scales, w1, w2, offs, out):
             size = WIDTH[kind]
             for d in shape[1:]:
                 size = size * d
-            size = max((size + 63) // 64 * 64, room)
+            size = max((size + ALIGN - 1) // ALIGN * ALIGN, room)
             if isinstance(on, list):
                 on = [x for x in on if x == "fresh" or spans[x][0] + size <= spans[x][1]][0]
             at = spans[on][0]
             spans[on][0] = at + size
             assert on == "fresh" or spans[on][0] <= spans[on][1], name
             spans[name] = [at, at + size]
-            return arena.tile(shape, DTYPE[kind], name=name, align_bytes=64, offset=at)
+            return arena.tile(shape, DTYPE[kind], name=name, align_bytes=ALIGN, offset=at)
 
-        offsets = held.tile([P, E * LIST_COLS], U16, name="offsets")
-        tok_words = [held.tile([P, T], I32, name="tok_words%d" % o, align_bytes=64) for o in range(PASSES)]
-        tok_scales = held.tile([P, T], U8, name="tok_scales", align_bytes=64)
+        offsets = held.tile([P, E * LIST_COLS], U16, name="offsets", align_bytes=ALIGN)
+        tok_words = [held.tile([P, T], I32, name="tok_words%d" % o, align_bytes=ALIGN) for o in range(PASSES)]
+        tok_scales = held.tile([P, T], U8, name="tok_scales", align_bytes=ALIGN)
         zero = held.tile([P, 1], F32, name="zero")
         bias = held.tile([P, 1], F32, name="bias")
         w1_raw = [place("w1_raw%d" % n, [P, PACK, H], "f32") for n in range(LAST + 1)]

@@ -74,11 +74,11 @@ def tile_moe_pke_mlp_gelu_kernel(tc, x_words, x_scales, w1, w2, offs, out):
         def load_words(o):
             nc.sync.dma_start(out=tok_words[o][:], in_=x_words[o].rearrange("p n r -> p (n r)").bitcast(I32))
 
-        def load_scales():
-            for q in range(4):
+        def load_scales(o):
+            for r in range(4):
                 nc.sync.dma_start(
-                    out=tok_scales[32 * q : 32 * q + 4 * PASSES, :].bitcast(I32),
-                    in_=x_scales[:, 4 * q : 4 * q + 4, :].bitcast(I32),
+                    out=tok_scales[4 * o + r : P : 32, :].bitcast(I32),
+                    in_=x_scales[o, r : 16 : 4, :].bitcast(I32),
                 )
 
         def load_w1(n):
@@ -96,9 +96,11 @@ def tile_moe_pke_mlp_gelu_kernel(tc, x_words, x_scales, w1, w2, offs, out):
 
         nc.sync.dma_start(offsets[:], offs)
         load_words(0)
-        load_scales()
+        load_scales(0)
         for n in range(LAST + 1):
             load_w1(n)
+            if n == 1:
+                load_scales(1)
             if n == 3:
                 load_words(1)
         for g in W2_LOADS:
@@ -335,7 +337,7 @@ def tile_moe_pke_mlp_gelu_kernel(tc, x_words, x_scales, w1, w2, offs, out):
         for n in range(4):
             round_w1(n, nc.scalar.copy, whole, "fresh")
         quantise_w1(0, 0)
-        quantise_w1(1, 0)
+        quantise_w1(1, 0, raw(2))
         quantise_w1(2, 0)
         for g in range(E // 2):
             gather_words(g, 1)
@@ -394,12 +396,12 @@ def tile_moe_pke_mlp_gelu_kernel(tc, x_words, x_scales, w1, w2, offs, out):
         finish(3)
         warm_up(w2_mx[3])
         copy_out(2, 2, nc.scalar.copy, old(LAST))
-        quantise_h(E - 1, 0, "w2_stage3")
         for pair in ((4, 5), (6, 7)):
             for e in pair:
                 round_w2(e, nc.vector.tensor_copy, old(LAST))
             finish(pair[0])
             if pair[1] < E - 1:
+                quantise_h(E - 1, 0, "w2_raw4")
                 finish(pair[1])
                 quantise_h(E - 1, 1, "w2_stage4")
         quantise_w2(E - 1)

@@ -94,13 +94,12 @@ def tile_moe_pke_mlp_gelu_kernel(tc, x_words, x_scales, w1, w2, offs, out):
                 in_=w2[g[0] : g[-1] + 1].rearrange("e (p j) n -> p e (j n)", j=PACK),
             )
 
-        nc.sync.dma_start(offsets[:], offs)
         load_words(0)
-        load_scales(0)
+        nc.sync.dma_start(offsets[:], offs)
         for n in range(LAST + 1):
             load_w1(n)
-            if n == 1:
-                load_scales(1)
+            if n < PASSES:
+                load_scales(n)
             if n == 3:
                 load_words(1)
         for g in W2_LOADS:
@@ -298,17 +297,14 @@ def tile_moe_pke_mlp_gelu_kernel(tc, x_words, x_scales, w1, w2, offs, out):
 
         on_vector = (nc.vector.tensor_copy, nc.vector.tensor_copy)
 
-        def quantise_h_both(e, on):
-            if e < WIDE:
-                for r in range(R):
-                    h_bf[(e, r)] = place("h_bf%d_%d" % (e, r), [P, U * PACK], "bf16", on)
-                    nc.vector.tensor_copy(
-                        out=h_bf[(e, r)][:].bitcast(F32).rearrange("p (u a) -> p u a", a=2),
-                        in_=h_pairs[e][:].rearrange("p a c -> p (a c)").bitcast(F32).rearrange("p (a u) -> p u a", a=2)[:, r * U : (r + 1) * U, :],
-                    )
-                on = "fresh"
-            for r in range(R):
-                quantise_h(e, r, on)
+        def weave_and_quantise(e, on):
+            woven = place("h_bf%d" % e, [P, C * PACK], "bf16", on)
+            nc.vector.tensor_copy(
+                out=woven[:].bitcast(F32).rearrange("p (u a) -> p u a", a=2),
+                in_=h_pairs[e][:].rearrange("p a c -> p (a c)").bitcast(F32).rearrange("p (a u) -> p u a", a=2),
+            )
+            h_mx[e] = (place("h_codes%d" % e, [P, C], "u32"), place("h_scales%d" % e, [P, C], "u8"))
+            quantise(woven[:], h_mx[e][0][:], h_mx[e][1][:])
 
         def warm_up(stationary):
             spare = psum.tile([P, 2 * C], F32, name="bank")
@@ -324,11 +320,14 @@ def tile_moe_pke_mlp_gelu_kernel(tc, x_words, x_scales, w1, w2, offs, out):
                 )
 
         def vector_pass(n):
-            round_halves(n, on_vector)
-            quantise_w1(n, 0, old(n))
-            if (n - 1, 0) not in w1_mx:
-                quantise_w1(n - 1, 0, raw(n))
-            quantise_w1(n, 2, old(n))
+            if n < LAST - 3:
+                round_w1(n, nc.vector.tensor_copy, whole, old(n))
+                if (n - 1, 0) not in w1_mx:
+                    quantise_w1(n - 1, 0, raw(n))
+                quantise_w1(n, 0, old(n))
+            else:
+                round_halves(n, on_vector)
+                quantise_halves(n)
 
         for g in range(E // 2):
             gather_words(g, 0)
@@ -353,8 +352,8 @@ def tile_moe_pke_mlp_gelu_kernel(tc, x_words, x_scales, w1, w2, offs, out):
         vector_pass(6)
         products(2)
         gelu(2, old(6))
-        quantise_h_both(0, "stage6_0")
-        quantise_h_both(1, "stage6_2")
+        weave_and_quantise(0, "stage6_0")
+        weave_and_quantise(1, "stage6_0")
         vector_pass(7)
         products(3)
         for e in range(4, E - 1):
@@ -368,8 +367,8 @@ def tile_moe_pke_mlp_gelu_kernel(tc, x_words, x_scales, w1, w2, offs, out):
             vector_pass(n + 1)
             products(e)
             if e == 4:
-                quantise_h_both(2, "stage%d_0" % (n + 1))
-            quantise_h_both(e - 1, "stage%d_2" % (n + 1) if e == 4 else "stage%d_0" % (n + 1))
+                weave_and_quantise(2, "stage%d_0" % (n + 1))
+            weave_and_quantise(e - 1, "stage%d_0" % (n + 1))
         gelu(E - 2, old(LAST))
         vector_pass(LAST - 1)
         warm_up(w1_mx[(LAST - 1, PACK - 1)])

@@ -26,7 +26,7 @@ LIST_COLS = C // 16
 LAST = PASSES * E - 1
 ALIGN = 256
 
-WIDE = 6
+WIDE = 7
 EARLY = 0
 W2_ON_SCALAR = (3, 4)
 W2_LOADS = [(0,), (1,), (2,), (3,), (4, 5), (6, 7)]
@@ -298,12 +298,13 @@ def tile_moe_pke_mlp_gelu_kernel(tc, x_words, x_scales, w1, w2, offs, out):
         on_vector = (nc.vector.tensor_copy, nc.vector.tensor_copy)
 
         def weave_and_quantise(e, on):
-            woven = place("h_bf%d" % e, [P, C * PACK], "bf16", on)
-            nc.vector.tensor_copy(
+            woven = place("h_bf%d" % e, [P, C * PACK], "bf16", old(LAST - 2) if e >= WIDE - 2 else on)
+            copy = nc.scalar.copy if e >= WIDE - 2 else nc.vector.tensor_copy
+            copy(
                 out=woven[:].bitcast(F32).rearrange("p (u a) -> p u a", a=2),
                 in_=h_pairs[e][:].rearrange("p a c -> p (a c)").bitcast(F32).rearrange("p (a u) -> p u a", a=2),
             )
-            h_mx[e] = (place("h_codes%d" % e, [P, C], "u32"), place("h_scales%d" % e, [P, C], "u8"))
+            h_mx[e] = (place("h_codes%d" % e, [P, C], "u32", on if e >= WIDE - 2 else "fresh"), place("h_scales%d" % e, [P, C], "u8"))
             quantise(woven[:], h_mx[e][0][:], h_mx[e][1][:])
 
         def warm_up(stationary):
@@ -381,11 +382,10 @@ def tile_moe_pke_mlp_gelu_kernel(tc, x_words, x_scales, w1, w2, offs, out):
         round_w2(0, nc.vector.tensor_copy, old(LAST))
         quantise_w1(LAST, 0, old(LAST))
         finish(0)
-        quantise_h(E - 2, 0, "stage%d_0" % LAST)
         quantise_w1(LAST, 2, old(LAST))
         for e in (1, 2):
             round_w2(e, nc.scalar.copy, old(LAST))
-        quantise_h(E - 2, 1, old(LAST))
+        weave_and_quantise(E - 2, "stage%d_0" % LAST)
         finish(1)
         products(E - 1)
         gelu(E - 1, old(LAST))
@@ -400,10 +400,10 @@ def tile_moe_pke_mlp_gelu_kernel(tc, x_words, x_scales, w1, w2, offs, out):
                 round_w2(e, nc.vector.tensor_copy, old(LAST))
             finish(pair[0])
             if pair[1] < E - 1:
-                quantise_h(E - 1, 0, "w2_raw4")
                 finish(pair[1])
-                quantise_h(E - 1, 1, "w2_stage4")
+                quantise_h(E - 1, 0, "w2_stage4")
         quantise_w2(E - 1)
+        quantise_h(E - 1, 1, "w2_stage%d" % (E - 2))
         copy_out(4, 2, nc.scalar.copy, old(LAST))
         copy_out(6, 1, nc.scalar.copy, old(LAST))
         y_last = place("y_last", [P, R, U], "f32", old(LAST))

@@ -372,7 +372,6 @@ def tile_moe_pke_mlp_gelu_kernel(tc, x_words, x_scales, w1, w2, offs, out):
             weave_and_quantise(e - 1, "stage%d_0" % (n + 1))
         gelu(E - 2, old(LAST))
         vector_pass(LAST - 1)
-        warm_up(w1_mx[(LAST - 1, PACK - 1)])
 
         def finish(e):
             quantise_w2(e)
@@ -393,7 +392,6 @@ def tile_moe_pke_mlp_gelu_kernel(tc, x_words, x_scales, w1, w2, offs, out):
         round_w2(3, nc.vector.tensor_copy, old(LAST))
         finish(2)
         finish(3)
-        warm_up(w2_mx[3])
         copy_out(2, 2, nc.scalar.copy, old(LAST))
         for pair in ((4, 5), (6, 7)):
             for e in pair:

@@ -98,9 +98,9 @@ def tile_moe_pke_mlp_gelu_kernel(tc, x_words, x_scales, w1, w2, offs, out):
         nc.sync.dma_start(offsets[:], offs)
         for n in range(LAST + 1):
             load_w1(n)
-            if n < PASSES:
-                load_scales(n)
-            if n == 3:
+            if n in (1, 2):
+                load_scales(n - 1)
+            if n == 1:
                 load_words(1)
         for g in W2_LOADS:
             load_w2(g)
@@ -332,15 +332,15 @@ def tile_moe_pke_mlp_gelu_kernel(tc, x_words, x_scales, w1, w2, offs, out):
 
         for g in range(E // 2):
             gather_words(g, 0)
-        for g in range(E // 2):
-            gather_scales(g)
         for n in range(4):
             round_w1(n, nc.scalar.copy, whole, "fresh")
         quantise_w1(0, 0)
-        quantise_w1(1, 0, raw(2))
-        quantise_w1(2, 0)
         for g in range(E // 2):
             gather_words(g, 1)
+        quantise_w1(1, 0, raw(2))
+        for g in range(E // 2):
+            gather_scales(g)
+        quantise_w1(2, 0, raw(3))
         products(0)
         quantise_w1(3, 0)
         products(1)

@@ -396,14 +396,28 @@ def tile_moe_pke_mlp_gelu_kernel(tc, x_words, x_scales, w1, w2, offs, out):
         for pair in ((4, 5), (6, 7)):
             for e in pair:
                 round_w2(e, nc.vector.tensor_copy, old(LAST))
-            finish(pair[0])
             if pair[1] < E - 1:
+                finish(pair[0])
                 finish(pair[1])
-                quantise_h(E - 1, 0, "w2_stage4")
+        quantise_w2(E - 2)
+        quantise_h(E - 1, 0, "w2_stage4")
         quantise_w2(E - 1)
         quantise_h(E - 1, 1, "w2_stage%d" % (E - 2))
         copy_out(4, 2, nc.scalar.copy, old(LAST))
-        copy_out(6, 1, nc.scalar.copy, old(LAST))
+        y_before = place("y_before", [P, R, U], "f32", old(LAST))
+        for r, copy in enumerate((nc.scalar.copy, nc.vector.tensor_copy)):
+            bank = psum.tile([P, U], F32, name="bank")
+            nc.tensor.matmul_mx(
+                out=bank[:],
+                lhsT=w2_mx[E - 2][0].bitcast(FP8X4),
+                lhsT_scale=w2_mx[E - 2][1],
+                rhs=h_mx[E - 2][0][:, r * U : (r + 1) * U].bitcast(FP8X4),
+                rhs_scale=h_mx[E - 2][1][:, r * U : (r + 1) * U],
+                start=True,
+                stop=True,
+            )
+            copy(out=y_before[:, r, :], in_=bank[:])
+        nc.sync.dma_start(out=out.rearrange("n (r c) -> n r c", r=R)[:, :, (E - 2) * U : (E - 1) * U], in_=y_before[:])
         y_last = place("y_last", [P, R, U], "f32", old(LAST))
         last_product(0, nc.scalar.copy)
         last_product(1, nc.vector.tensor_copy)

@@ -27,6 +27,9 @@ LAST = PASSES * E - 1
 ALIGN = 256
 
 WIDE = 7
+GROUP = 4
+WINDOW = 1408
+GROUPS = 2
 EARLY = 0
 W2_ON_SCALAR = (3, 4)
 W2_LOADS = [(0,), (1,), (2,), (3,), (4, 5), (6, 7)]
@@ -56,28 +59,31 @@ def tile_moe_pke_mlp_gelu_kernel(tc, x_words, x_scales, w1, w2, offs, out):
             return arena.tile(shape, DTYPE[kind], name=name, align_bytes=ALIGN, offset=at)
 
         offsets = held.tile([P, E * LIST_COLS], U16, name="offsets", align_bytes=ALIGN)
-        tok_words = [held.tile([P, T], I32, name="tok_words%d" % o, align_bytes=ALIGN) for o in range(PASSES)]
-        tok_scales = held.tile([P, T], U8, name="tok_scales", align_bytes=ALIGN)
+        tok_words = [held.tile([P, WINDOW], I32, name="tok_words%d" % o, align_bytes=ALIGN) for o in range(PASSES)]
+        tok_scales = held.tile([P, WINDOW], U8, name="tok_scales", align_bytes=ALIGN)
         zero = held.tile([P, 1], F32, name="zero")
         bias = held.tile([P, 1], F32, name="bias")
         w1_raw = [place("w1_raw%d" % n, [P, PACK, H], "f32") for n in range(LAST + 1)]
+        spans["raw_spare"] = [spans["w1_raw12"][0], spans["w1_raw12"][1]]
         w2_raw = {}
         for g in W2_LOADS:
             both = place("w2_raw%d" % g[0], [P, len(g), PACK, N], "f32")
             for i, e in enumerate(g):
                 w2_raw[e] = (both, i)
 
-        nc.vector.memset(tok_scales[:].bitcast(I32), 0)
-        nc.vector.memset(zero[:], 0.0)
+        nc.gpsimd.memset(tok_scales[:].bitcast(I32), 0)
+        nc.gpsimd.memset(zero[:], 0.0)
+        for o in range(PASSES):
+            nc.gpsimd.memset(tok_words[o][:, T:], 0)
         nc.scalar.activation(out=bias[:], in_=zero[:], func=GELU)
 
         def load_words(o):
-            nc.sync.dma_start(out=tok_words[o][:], in_=x_words[o].rearrange("p n r -> p (n r)").bitcast(I32))
+            nc.sync.dma_start(out=tok_words[o][:, :T], in_=x_words[o].rearrange("p n r -> p (n r)").bitcast(I32))
 
         def load_scales(o):
             for r in range(4):
                 nc.sync.dma_start(
-                    out=tok_scales[4 * o + r : P : 32, :].bitcast(I32),
+                    out=tok_scales[4 * o + r : P : 32, :T].bitcast(I32),
                     in_=x_scales[o, r : 16 : 4, :].bitcast(I32),
                 )
 
@@ -122,14 +128,17 @@ def tile_moe_pke_mlp_gelu_kernel(tc, x_words, x_scales, w1, w2, offs, out):
         def quantise(src, codes, scales):
             nc.vector.quantize_mx(out=codes.bitcast(FP8X4), scales=scales, in_=src)
 
+        def group(g):
+            return range(GROUP * g, min(GROUP * (g + 1), E))
+
         def gather_words(g, o, on="fresh"):
-            cols = slice(2 * g * LIST_COLS, 2 * (g + 1) * LIST_COLS)
-            slot_words[(g, o)] = place("slot_words%d_%d" % (g, o), [P, 2 * C], "u32", on)
+            cols = slice(group(g).start * LIST_COLS, group(g).stop * LIST_COLS)
+            slot_words[(g, o)] = place("slot_words%d_%d" % (g, o), [P, len(group(g)) * C], "u32", on)
             nc.vector.tensor_copy(out=slot_words[(g, o)][:], in_=tok_words[o][:].bitcast(U32).indirect(offsets[:, cols]))
 
         def gather_scales(g):
-            cols = slice(2 * g * LIST_COLS, 2 * (g + 1) * LIST_COLS)
-            slot_scales[g] = place("slot_scales%d" % g, [P, 2 * C], "u8")
+            cols = slice(group(g).start * LIST_COLS, group(g).stop * LIST_COLS)
+            slot_scales[g] = place("slot_scales%d" % g, [P, len(group(g)) * C], "u8")
             nc.vector.tensor_copy(out=slot_scales[g][:], in_=tok_scales[:].indirect(offsets[:, cols]))
 
         def round_w1(n, copy, ts, on):
@@ -163,7 +172,7 @@ def tile_moe_pke_mlp_gelu_kernel(tc, x_words, x_scales, w1, w2, offs, out):
 
         def wide_product(e, a):
             a_banks[(e, a)] = psum.tile([P, 2, C], F32, name="bank")
-            ncols = slice((e % 2) * C, (e % 2 + 1) * C)
+            ncols = slice((e % GROUP) * C, (e % GROUP + 1) * C)
             for t in range(2):
                 for o in range(PASSES):
                     wc, ws = w1_mx[(PASSES * e + o, 2 * a + t)]
@@ -171,8 +180,8 @@ def tile_moe_pke_mlp_gelu_kernel(tc, x_words, x_scales, w1, w2, offs, out):
                         out=a_banks[(e, a)][:, t, :],
                         lhsT=wc.bitcast(FP8X4),
                         lhsT_scale=ws,
-                        rhs=slot_words[(e // 2, o)][:, ncols].bitcast(FP8X4),
-                        rhs_scale=slot_scales[e // 2][4 * o : P, ncols],
+                        rhs=slot_words[(e // GROUP, o)][:, ncols].bitcast(FP8X4),
+                        rhs_scale=slot_scales[e // GROUP][4 * o : P, ncols],
                         start=(o == 0),
                         stop=(o == PASSES - 1),
                     )
@@ -187,7 +196,7 @@ def tile_moe_pke_mlp_gelu_kernel(tc, x_words, x_scales, w1, w2, offs, out):
 
         def first_product(e, r):
             a_banks[(e, r)] = psum.tile([P, PACK, U], F32, name="bank")
-            ncols = slice((e % 2) * C + r * U, (e % 2) * C + (r + 1) * U)
+            ncols = slice((e % GROUP) * C + r * U, (e % GROUP) * C + (r + 1) * U)
             for t in range(PACK):
                 for o in range(PASSES):
                     wc, ws = w1_mx[(PASSES * e + o, t)]
@@ -195,8 +204,8 @@ def tile_moe_pke_mlp_gelu_kernel(tc, x_words, x_scales, w1, w2, offs, out):
                         out=a_banks[(e, r)][:, t, :],
                         lhsT=wc.bitcast(FP8X4),
                         lhsT_scale=ws,
-                        rhs=slot_words[(e // 2, o)][:, ncols].bitcast(FP8X4),
-                        rhs_scale=slot_scales[e // 2][4 * o : P, ncols],
+                        rhs=slot_words[(e // GROUP, o)][:, ncols].bitcast(FP8X4),
+                        rhs_scale=slot_scales[e // GROUP][4 * o : P, ncols],
                         start=(o == 0),
                         stop=(o == PASSES - 1),
                     )
@@ -307,19 +316,6 @@ def tile_moe_pke_mlp_gelu_kernel(tc, x_words, x_scales, w1, w2, offs, out):
             h_mx[e] = (place("h_codes%d" % e, [P, C], "u32", on if e >= WIDE - 2 else "fresh"), place("h_scales%d" % e, [P, C], "u8"))
             quantise(woven[:], h_mx[e][0][:], h_mx[e][1][:])
 
-        def warm_up(stationary):
-            spare = psum.tile([P, 2 * C], F32, name="bank")
-            for repeat in range(2):
-                nc.tensor.matmul_mx(
-                    out=spare[:],
-                    lhsT=stationary[0].bitcast(FP8X4),
-                    lhsT_scale=stationary[1],
-                    rhs=slot_words[(E // 2 - 1, 0)][:].bitcast(FP8X4),
-                    rhs_scale=slot_scales[E // 2 - 1][:],
-                    start=True,
-                    stop=True,
-                )
-
         def vector_pass(n):
             if n < LAST - 3:
                 round_w1(n, nc.vector.tensor_copy, whole, old(n))
@@ -330,15 +326,15 @@ def tile_moe_pke_mlp_gelu_kernel(tc, x_words, x_scales, w1, w2, offs, out):
                 round_halves(n, on_vector)
                 quantise_halves(n)
 
-        for g in range(E // 2):
+        for g in range(GROUPS):
             gather_words(g, 0)
         for n in range(4):
             round_w1(n, nc.scalar.copy, whole, "fresh")
         quantise_w1(0, 0)
-        for g in range(E // 2):
+        for g in range(GROUPS):
             gather_words(g, 1)
         quantise_w1(1, 0, raw(2))
-        for g in range(E // 2):
+        for g in range(GROUPS):
             gather_scales(g)
         quantise_w1(2, 0, raw(3))
         products(0)
@@ -374,7 +370,7 @@ def tile_moe_pke_mlp_gelu_kernel(tc, x_words, x_scales, w1, w2, offs, out):
         vector_pass(LAST - 1)
 
         def finish(e):
-            quantise_w2(e)
+            quantise_w2(e, "raw_spare")
             second_product(e)
 
         round_halves(LAST, (nc.vector.tensor_copy, nc.scalar.copy))

from contextlib import ExitStack

import concourse.mybir as mybir

K, T, E, C, H, N = 1024, 1024, 8, 256, 512, 128
R = 2
FLOPS = 2 * E * C * (K * H + H * N)

F32 = mybir.dt.float32
BF16 = mybir.dt.bfloat16
I32 = mybir.dt.int32
U32 = mybir.dt.uint32
U16 = mybir.dt.uint16
U8 = mybir.dt.uint8
FP8X4 = mybir.dt.float8_e4m3fn_x4
GELU = mybir.ActivationFunctionType.Gelu_apprx_tanh
WIDTH = {"f32": 4, "bf16": 2, "u32": 4, "u8": 1}
DTYPE = {"f32": F32, "bf16": BF16, "u32": U32, "u8": U8}

P = 128
PACK = 4
K_PASS = P * PACK
PASSES = K // K_PASS
U = C // R
LIST_COLS = C // 16
LAST = PASSES * E - 1
ALIGN = 256

WIDE = 7
GROUP = 4
WINDOW = 1408
GROUPS = 2
EARLY = 0
W2_ON_SCALAR = (3, 4)
W2_LOADS = [(0,), (1,), (2,), (3,), (4, 5), (6, 7)]
OUT_GROUPS = [(0, 1), (2, 3), (4, 5), (6,), (7,)]


def tile_moe_pke_mlp_gelu_kernel(tc, x_words, x_scales, w1, w2, offs, out):
    nc = tc.nc
    with ExitStack() as ctx:
        held = ctx.enter_context(tc.tile_pool(name="held", bufs=1))
        arena = ctx.enter_context(tc.tile_pool(name="arena", bufs=1))
        psum = ctx.enter_context(tc.psum_pool(name="psum", bufs=8))

        spans = {"fresh": [0, 0]}

        def place(name, shape, kind, on="fresh", room=0):
            size = WIDTH[kind]
            for d in shape[1:]:
                size = size * d
            size = max((size + ALIGN - 1) // ALIGN * ALIGN, room)
            if isinstance(on, list):
                on = [x for x in on if x == "fresh" or spans[x][0] + size <= spans[x][1]][0]
            at = spans[on][0]
            spans[on][0] = at + size
            assert on == "fresh" or spans[on][0] <= spans[on][1], name
            spans[name] = [at, at + size]
            return arena.tile(shape, DTYPE[kind], name=name, align_bytes=ALIGN, offset=at)

        offsets = held.tile([P, E * LIST_COLS], U16, name="offsets", align_bytes=ALIGN)
        tok_words = [held.tile([P, WINDOW], I32, name="tok_words%d" % o, align_bytes=ALIGN) for o in range(PASSES)]
        tok_scales = held.tile([P, WINDOW], U8, name="tok_scales", align_bytes=ALIGN)
        zero = held.tile([P, 1], F32, name="zero")
        bias = held.tile([P, 1], F32, name="bias")
        w1_raw = [place("w1_raw%d" % n, [P, PACK, H], "f32") for n in range(LAST + 1)]
        spans["raw_spare"] = [spans["w1_raw12"][0], spans["w1_raw12"][1]]
        w2_raw = {}
        for g in W2_LOADS:
            both = place("w2_raw%d" % g[0], [P, len(g), PACK, N], "f32")
            for i, e in enumerate(g):
                w2_raw[e] = (both, i)

        nc.gpsimd.memset(tok_scales[:].bitcast(I32), 0)
        nc.gpsimd.memset(zero[:], 0.0)
        for o in range(PASSES):
            nc.gpsimd.memset(tok_words[o][:, T:], 0)
        nc.scalar.activation(out=bias[:], in_=zero[:], func=GELU)

        def load_words(o):
            nc.sync.dma_start(out=tok_words[o][:, :T], in_=x_words[o].rearrange("p n r -> p (n r)").bitcast(I32))

        def load_scales(o):
            for r in range(4):
                nc.sync.dma_start(
                    out=tok_scales[4 * o + r : P : 32, :T].bitcast(I32),
                    in_=x_scales[o, r : 16 : 4, :].bitcast(I32),
                )

        def load_w1(n):
            e, o = divmod(n, PASSES)
            nc.sync.dma_start(
                out=w1_raw[n][:],
                in_=w1[e, o * K_PASS : (o + 1) * K_PASS, :].rearrange("(p j) c -> p j c", j=PACK),
            )

        def load_w2(g):
            nc.sync.dma_start(
                out=w2_raw[g[0]][0][:].rearrange("p e j n -> p e (j n)"),
                in_=w2[g[0] : g[-1] + 1].rearrange("e (p j) n -> p e (j n)", j=PACK),
            )

        load_words(0)
        nc.sync.dma_start(offsets[:], offs)
        for n in range(LAST + 1):
            load_w1(n)
            if n in (1, 2):
                load_scales(n - 1)
            if n == 1:
                load_words(1)
        for g in W2_LOADS:
            load_w2(g)

        stage = {}
        slot_words = {}
        slot_scales = {}
        w1_mx = {}
        w2_stage = {}
        w2_mx = {}
        h_bf = {}
        h_mx = {}
        h_pairs = {}
        a_banks = {}
        y_banks = {}
        y_of = {}
        y_sb = {}

        def quantise(src, codes, scales):
            nc.vector.quantize_mx(out=codes.bitcast(FP8X4), scales=scales, in_=src)

        def group(g):
            return range(GROUP * g, min(GROUP * (g + 1), E))

        def gather_words(g, o, on="fresh"):
            cols = slice(group(g).start * LIST_COLS, group(g).stop * LIST_COLS)
            slot_words[(g, o)] = place("slot_words%d_%d" % (g, o), [P, len(group(g)) * C], "u32", on)
            nc.vector.tensor_copy(out=slot_words[(g, o)][:], in_=tok_words[o][:].bitcast(U32).indirect(offsets[:, cols]))

        def gather_scales(g):
            cols = slice(group(g).start * LIST_COLS, group(g).stop * LIST_COLS)
            slot_scales[g] = place("slot_scales%d" % g, [P, len(group(g)) * C], "u8")
            nc.vector.tensor_copy(out=slot_scales[g][:], in_=tok_scales[:].indirect(offsets[:, cols]))

        def round_w1(n, copy, ts, on):
            name = "stage%d_%d" % (n, ts.start)
            tile = place(name, [P, ts.stop - ts.start, P * PACK], "bf16", on)
            stage[(n, ts.start)] = (tile, ts)
            src = w1_raw[n][:].rearrange("p j (m t) -> p m j t", t=PACK)
            copy(out=tile[:].rearrange("p t (m j) -> p m j t", j=PACK), in_=src[:, :, :, ts])

        def quantise_w1(n, first, on="fresh"):
            tile, ts = stage[(n, first)]
            count = ts.stop - ts.start
            codes = place("w1_codes%d_%d" % (n, first), [P, count * P], "u32", on)
            scales = place("w1_scales%d_%d" % (n, first), [P, count * P], "u8", on)
            quantise(tile[:].rearrange("p t c -> p (t c)"), codes[:], scales[:])
            for t in range(count):
                w1_mx[(n, first + t)] = (codes[:, t * P : (t + 1) * P], scales[:, t * P : (t + 1) * P])

        def round_w2(e, copy, on):
            w2_stage[e] = place("w2_stage%d" % e, [P, N * PACK], "bf16", on, 2048)
            copy(
                out=w2_stage[e][:].rearrange("p (c i j) -> p c j i", i=4, j=PACK),
                in_=w2_raw[e][0][:, w2_raw[e][1], :, :].rearrange("p j (c i) -> p c j i", i=4),
            )

        def quantise_w2(e, on="fresh"):
            codes = place("w2_codes%d" % e, [P, N], "u32", on)
            scales = place("w2_scales%d" % e, [P, N], "u8", on)
            quantise(w2_stage[e][:], codes[:], scales[:])
            w2_mx[e] = (codes[:], scales[:])

        def wide_product(e, a):
            a_banks[(e, a)] = psum.tile([P, 2, C], F32, name="bank")
            ncols = slice((e % GROUP) * C, (e % GROUP + 1) * C)
            for t in range(2):
                for o in range(PASSES):
                    wc, ws = w1_mx[(PASSES * e + o, 2 * a + t)]
                    nc.tensor.matmul_mx(
                        out=a_banks[(e, a)][:, t, :],
                        lhsT=wc.bitcast(FP8X4),
                        lhsT_scale=ws,
                        rhs=slot_words[(e // GROUP, o)][:, ncols].bitcast(FP8X4),
                        rhs_scale=slot_scales[e // GROUP][4 * o : P, ncols],
                        start=(o == 0),
                        stop=(o == PASSES - 1),
                    )

        def wide_activate(e, a):
            nc.scalar.activation(
                out=h_pairs[e][:, a, :].rearrange("p (u t) -> p u t", t=2),
                in_=a_banks[(e, a)][:].rearrange("p t u -> p u t"),
                func=GELU,
                bias=bias[:],
            )

        def first_product(e, r):
            a_banks[(e, r)] = psum.tile([P, PACK, U], F32, name="bank")
            ncols = slice((e % GROUP) * C + r * U, (e % GROUP) * C + (r + 1) * U)
            for t in range(PACK):
                for o in range(PASSES):
                    wc, ws = w1_mx[(PASSES * e + o, t)]
                    nc.tensor.matmul_mx(
                        out=a_banks[(e, r)][:, t, :],
                        lhsT=wc.bitcast(FP8X4),
                        lhsT_scale=ws,
                        rhs=slot_words[(e // GROUP, o)][:, ncols].bitcast(FP8X4),
                        rhs_scale=slot_scales[e // GROUP][4 * o : P, ncols],
                        start=(o == 0),
                        stop=(o == PASSES - 1),
                    )

        def activate(e, r, on):
            h_bf[(e, r)] = place("h_bf%d_%d" % (e, r), [P, U * PACK], "bf16", on)
            nc.scalar.activation(
                out=h_bf[(e, r)][:].rearrange("p (u t) -> p u t", t=PACK),
                in_=a_banks[(e, r)][:].rearrange("p t u -> p u t"),
                func=GELU,
                bias=bias[:],
            )

        def quantise_h(e, r, on="fresh"):
            key = (e, r) if e == E - 1 else e
            width = U if e == E - 1 else C
            if key not in h_mx:
                name = "%d_%d" % (e, r)
                h_mx[key] = (place("h_codes" + name, [P, width], "u32", on), place("h_scales" + name, [P, width], "u8", on))
            cols = slice(0, U) if e == E - 1 else slice(r * U, (r + 1) * U)
            quantise(h_bf[(e, r)][:], h_mx[key][0][:, cols], h_mx[key][1][:, cols])

        def last_product(r, copy):
            bank = psum.tile([P, U], F32, name="bank")
            nc.tensor.matmul_mx(
                out=bank[:],
                lhsT=w2_mx[E - 1][0].bitcast(FP8X4),
                lhsT_scale=w2_mx[E - 1][1],
                rhs=h_mx[(E - 1, r)][0][:].bitcast(FP8X4),
                rhs_scale=h_mx[(E - 1, r)][1][:],
                start=True,
                stop=True,
            )
            copy(out=y_last[:, r, :], in_=bank[:])

        def second_product(e):
            pair = e // 2
            if pair not in y_banks or e == E - 1:
                y_banks[pair] = psum.tile([P, 2, R, U], F32, name="bank")
            y_of[e] = y_banks[pair]
            nc.tensor.matmul_mx(
                out=y_of[e][:, e % 2, :, :].rearrange("p r u -> p (r u)"),
                lhsT=w2_mx[e][0].bitcast(FP8X4),
                lhsT_scale=w2_mx[e][1],
                rhs=h_mx[e][0][:].bitcast(FP8X4),
                rhs_scale=h_mx[e][1][:],
                start=True,
                stop=True,
            )

        def copy_out(first, count, copy, on):
            g = [g for g in OUT_GROUPS if first in g][0]
            if g not in y_sb:
                y_sb[g] = place("y_sb%d" % g[0], [P, R, len(g), U], "f32", on)
            copy(
                out=y_sb[g][:, :, first - g[0] : first - g[0] + count, :],
                in_=y_of[first][:, first % 2 : first % 2 + count].rearrange("p e r u -> p r e u"),
            )
            if first + count - 1 == g[-1]:
                nc.sync.dma_start(
                    out=out.rearrange("n (r c) -> n r c", r=R)[:, :, g[0] * U : (g[-1] + 1) * U],
                    in_=y_sb[g][:].rearrange("p r e u -> p r (e u)"),
                )

        both = slice(0, R)
        halves = [slice(r, r + 1) for r in range(R)]
        whole = slice(0, PACK)

        def old(n):
            return ["w1_raw%d" % m for m in range(n - 3)] + ["fresh"]

        def raw(n):
            return "w1_raw%d" % n if n >= 0 else "fresh"

        def round_halves(n, copies):
            for half in range(2):
                round_w1(n, copies[half], slice(2 * half, 2 * half + 2), old(n))

        def quantise_halves(n):
            for first in (0, 2):
                quantise_w1(n, first, old(n))

        def products(e):
            for r in range(R):
                if e < WIDE:
                    wide_product(e, r)
                else:
                    first_product(e, r)

        def gelu(e, on):
            if e < WIDE:
                h_pairs[e] = place("h_pairs%d" % e, [P, 2, C * 2], "bf16", on)
            for r in range(R):
                if e < WIDE:
                    wide_activate(e, r)
                else:
                    activate(e, r, on)

        on_vector = (nc.vector.tensor_copy, nc.vector.tensor_copy)

        def weave_and_quantise(e, on):
            woven = place("h_bf%d" % e, [P, C * PACK], "bf16", old(LAST - 2) if e >= WIDE - 2 else on)
            copy = nc.scalar.copy if e >= WIDE - 2 else nc.vector.tensor_copy
            copy(
                out=woven[:].bitcast(F32).rearrange("p (u a) -> p u a", a=2),
                in_=h_pairs[e][:].rearrange("p a c -> p (a c)").bitcast(F32).rearrange("p (a u) -> p u a", a=2),
            )
            h_mx[e] = (place("h_codes%d" % e, [P, C], "u32", on if e >= WIDE - 2 else "fresh"), place("h_scales%d" % e, [P, C], "u8"))
            quantise(woven[:], h_mx[e][0][:], h_mx[e][1][:])

        def vector_pass(n):
            if n < LAST - 3:
                round_w1(n, nc.vector.tensor_copy, whole, old(n))
                if (n - 1, 0) not in w1_mx:
                    quantise_w1(n - 1, 0, raw(n))
                quantise_w1(n, 0, old(n))
            else:
                round_halves(n, on_vector)
                quantise_halves(n)

        for g in range(GROUPS):
            gather_words(g, 0)
        for n in range(4):
            round_w1(n, nc.scalar.copy, whole, "fresh")
        quantise_w1(0, 0)
        for g in range(GROUPS):
            gather_words(g, 1)
        quantise_w1(1, 0, raw(2))
        for g in range(GROUPS):
            gather_scales(g)
        quantise_w1(2, 0, raw(3))
        products(0)
        quantise_w1(3, 0)
        products(1)
        round_w1(4, nc.scalar.copy, whole, old(4))
        quantise_w1(4, 0)
        round_w1(5, nc.scalar.copy, whole, old(5))
        gelu(0, raw(5))
        gelu(1, raw(5))

        vector_pass(6)
        products(2)
        gelu(2, old(6))
        weave_and_quantise(0, "stage6_0")
        weave_and_quantise(1, "stage6_0")
        vector_pass(7)
        products(3)
        for e in range(4, E - 1):
            n = PASSES * e
            if e < E - 2:
                round_w1(n, nc.scalar.copy, whole, old(n))
            else:
                round_halves(n, (nc.vector.tensor_copy, nc.scalar.copy))
                quantise_halves(n)
            gelu(e - 1, old(n))
            vector_pass(n + 1)
            products(e)
            if e == 4:
                weave_and_quantise(2, "stage%d_0" % (n + 1))
            weave_and_quantise(e - 1, "stage%d_0" % (n + 1))
        gelu(E - 2, old(LAST))
        vector_pass(LAST - 1)

        def finish(e):
            quantise_w2(e, "raw_spare")
            second_product(e)

        round_halves(LAST, (nc.vector.tensor_copy, nc.scalar.copy))
        round_w2(0, nc.vector.tensor_copy, old(LAST))
        quantise_w1(LAST, 0, old(LAST))
        finish(0)
        quantise_w1(LAST, 2, old(LAST))
        for e in (1, 2):
            round_w2(e, nc.scalar.copy, old(LAST))
        weave_and_quantise(E - 2, "stage%d_0" % LAST)
        finish(1)
        products(E - 1)
        gelu(E - 1, old(LAST))
        copy_out(0, 2, nc.scalar.copy, old(LAST))
        round_w2(3, nc.vector.tensor_copy, old(LAST))
        finish(2)
        finish(3)
        copy_out(2, 2, nc.scalar.copy, old(LAST))
        for pair in ((4, 5), (6, 7)):
            for e in pair:
                round_w2(e, nc.vector.tensor_copy, old(LAST))
            if pair[1] < E - 1:
                finish(pair[0])
                finish(pair[1])
        quantise_w2(E - 2)
        quantise_h(E - 1, 0, "w2_stage4")
        quantise_w2(E - 1)
        quantise_h(E - 1, 1, "w2_stage%d" % (E - 2))
        copy_out(4, 2, nc.scalar.copy, old(LAST))
        y_before = place("y_before", [P, R, U], "f32", old(LAST))
        for r, copy in enumerate((nc.scalar.copy, nc.vector.tensor_copy)):
            bank = psum.tile([P, U], F32, name="bank")
            nc.tensor.matmul_mx(
                out=bank[:],
                lhsT=w2_mx[E - 2][0].bitcast(FP8X4),
                lhsT_scale=w2_mx[E - 2][1],
                rhs=h_mx[E - 2][0][:, r * U : (r + 1) * U].bitcast(FP8X4),
                rhs_scale=h_mx[E - 2][1][:, r * U : (r + 1) * U],
                start=True,
                stop=True,
            )
            copy(out=y_before[:, r, :], in_=bank[:])
        nc.sync.dma_start(out=out.rearrange("n (r c) -> n r c", r=R)[:, :, (E - 2) * U : (E - 1) * U], in_=y_before[:])
        y_last = place("y_last", [P, R, U], "f32", old(LAST))
        last_product(0, nc.scalar.copy)
        last_product(1, nc.vector.tensor_copy)
        nc.sync.dma_start(out=out.rearrange("n (r c) -> n r c", r=R)[:, :, (E - 1) * U : E * U], in_=y_last[:])
